import numpy as np, ml_dtypes
CORES = [48,51,52,55]
N = 4
BF = ml_dtypes.bfloat16
S, M, CAP, L = 512, 512, 192, 6
F = 16 // N
def tries(rng, same=False, few=False):
    kid = np.zeros((N, 8, M, 16), np.int32); words = {}; deep = {}
    tid = (rng.integers(1, 65536, (N, 8, M)) * (rng.random((N, 8, M)) < (0.0625 if few else 0.5))).astype(np.int32)
    for q in range(N):
        for g in range(8):
            no = [0, 1] + (2 + rng.permutation(M - 2)).tolist(); pl = rng.random(M).tolist(); cl = rng.integers(0, 16, M).tolist()
            k = kid[q, g]; w = {1: []}; up = []; m = 2; deep[q, g] = []
            for c in (q * F + rng.permutation(F)).tolist()[:1 if few else F]:
                p = 1
                for d in range(L):
                    e = c if d == 0 or same else cl[m]
                    k[no[p], e] = no[m]; w[m] = w[p] + [e]
                    if d < L - 1: up.append(m)
                    p = m; m += 1
                tid[q, g, no[p]] = rng.integers(1, 65536); deep[q, g].append(w[p])
            for m in range(m, M):
                p = up[int(pl[m] * len(up))]; e = cl[m]
                if k[no[p], e]: continue
                k[no[p], e] = no[m]; w[m] = w[p] + [e]
                if len(w[m]) < L: up.append(m)
            words[q, g] = [v for v in w.values() if v]
    tid[:, :, 0] = 0
    return kid.reshape(N, 8, 16 * M), tid, words, deep
def strings(rng, words):
    s = np.zeros((8, N * S), np.int64)
    for g in range(8):
        qs = rng.integers(0, N, N * S).tolist(); ms = rng.random(N * S).tolist(); a = []; i = 0
        while len(a) < N * S:
            v = words[qs[i], g]; a += v[int(ms[i] * len(v))]; i += 1
        s[g] = a[:N * S]
    return np.where(rng.random(s.shape) < 0.1, rng.integers(0, 16, s.shape), s)
def plant(rng, s, deep):
    keep = np.zeros(s.shape, bool)
    for r in range(N):
        for g in range(8):
            v = deep[int(rng.integers(0, N)), g]; j = (r * S + S - 1 - g % (L - 1) + np.arange(L)) % (N * S)
            s[g, j] = v[int(rng.integers(0, len(v)))]; keep[g, j] = True
    return keep
def fit(rng, s, keep, full=False):
    s = s.reshape(8, N, S).transpose(1, 0, 2).astype(np.int32); keep = keep.reshape(8, N, S).transpose(1, 0, 2)
    a, b = int(rng.integers(0, N)), int(rng.integers(0, 8))
    for r in range(N):
        for g in range(8):
            e = s[r, g]; own = e // F; have = np.bincount(own, minlength=N); low = np.bincount(own[keep[r, g]], minlength=N)
            o = rng.permutation(N); i = np.flatnonzero((o == a) if full and g == b else (o != r))[0]; o[[0, i]] = o[[i, 0]]
            want = low.copy() if full else np.minimum(have, CAP)
            if full or (r, g) == (a, b): want[o[0]] = CAP
            for q in np.roll(o, -1): want[q] = min(max(int(want[q]) + S - int(np.sum(want)), int(low[q])), CAP)
            sur = np.concatenate([rng.permutation(np.flatnonzero((own == q) & ~keep[r, g]))[:max(int(have[q] - want[q]), 0)] for q in range(N)])
            need = np.repeat(np.arange(N), np.maximum(want - have, 0))
            e[sur] = need * F + rng.integers(0, F, len(need))
    return np.ascontiguousarray(s)
def setup_inputs(rng):
    kid, tid, words, deep = tries(rng); s = strings(rng, words); keep = plant(rng, s, deep)
    return {"lett": fit(rng, s, keep), "kid": kid, "tid": tid}
def setup_inputs_full(rng):
    kid, tid, words, deep = tries(rng); s = strings(rng, words)
    lett = fit(rng, s, np.zeros(s.shape, bool), True)
    assert np.sum((lett // F)[..., None] == np.arange(N), axis=2).min(axis=0).max() == CAP
    return {"lett": lett, "kid": kid, "tid": tid}
def setup_inputs_runs(rng):
    kid, tid, words, deep = tries(rng, same=True)
    s = np.stack([np.repeat(rng.integers(0, 16, N * S), rng.integers(1, 13, N * S))[:N * S] for g in range(8)]); keep = plant(rng, s, deep)
    return {"lett": fit(rng, s, keep), "kid": kid, "tid": tid}
def setup_inputs_few(rng):
    kid, tid, words, deep = tries(rng, few=True); s = strings(rng, words); keep = plant(rng, s, deep)
    return {"lett": fit(rng, s, keep), "kid": kid, "tid": tid}
def setup_inputs_spread(rng):
    kid = (rng.integers(0, M, (N, 8, M, 16)) * (rng.random((N, 8, M, 16)) > 0.125)).astype(np.int32)
    kid[:, :, 0] = 0; kid[:, :, 1] *= (np.arange(16) // F == np.arange(N)[:, None])[:, None, :]
    tid = (rng.integers(0, 65536, (N, 8, M)) * (rng.random((N, 8, M)) < 0.3)).astype(np.int32); tid[:, :, 0] = 0; tid[:, :, M - 1] = 65535
    s = np.minimum(np.floor(rng.random((8, N * S)) ** 2 * 16), 15).astype(np.int64)
    return {"lett": fit(rng, s, np.zeros(s.shape, bool)), "kid": kid.reshape(N, 8, 16 * M), "tid": tid}
def check_inputs(d):
    bad = []; s, kid, tid = d["lett"], d["kid"], d["tid"]
    if s.min() < 0 or s.max() > 15: bad.append("letters")
    if ((s // F)[..., None] == np.arange(N)).sum(2).max() > CAP: bad.append("slots")
    if kid.min() < 0 or kid.max() >= M: bad.append("children")
    if kid[:, :, :16].any() or tid[:, :, 0].any(): bad.append("node 0")
    if (kid[:, :, 16:32] * (np.arange(16) // F != np.arange(N)[:, None])[:, None, :]).any(): bad.append("roots")
    if tid.min() < 0 or tid.max() > 65535: bad.append("ids")
    return bad
def reference(lett, kid, tid):
    s = np.concatenate(list(lett), axis=1).astype(np.int64)
    own = s // F; g = np.arange(8)[:, None]; node = np.ones(s.shape, np.int64); yl = np.zeros(s.shape, np.int64); yi = np.zeros(s.shape, np.int64)
    for k in range(L):
        node = kid[own, g, 16 * node + np.roll(s, -k, axis=1)].astype(np.int64)
        t = tid[own, g, node]
        yl = np.where(t > 0, k + 1, yl); yi = np.where(t > 0, t, yi)
    yl = np.ascontiguousarray(yl.reshape(8, N, S).transpose(1, 0, 2)); yi = np.ascontiguousarray(yi.reshape(8, N, S).transpose(1, 0, 2))
    return {"ylen": yl.astype(np.float32), "yid": yi.astype(np.float32)}

@@ -1,0 +1,258 @@
+from concourse.bass import DstId, RemoteDMATransfer
+from concourse.mybir import AluOpType, AxisListType, ActivationFunctionType
+
+SCRATCH = {
+    "KR": ("sbuf", [128, 2, 16, 16], "int32"),
+    "W": ("sbuf", [128, 2048], "int32"),
+    "IDW": ("sbuf", [128, 2048], "bfloat16"),
+    "L8": ("sbuf", [128, 512], "int32"),
+    "L8h": ("sbuf", [128, 512], "float16"),
+    "T8": ("sbuf", [128, 512], "int32"),
+    "T8f": ("sbuf", [128, 512], "float32"),
+    "H8": ("sbuf", [128, 512], "bfloat16"),
+    "F8": ("sbuf", [128, 512], "bfloat16"),
+    "Q8": ("sbuf", [128, 512], "bfloat16"),
+    "OH": ("sbuf", [128, 592], "float16"),
+    "HL": ("sbuf", [128, 80], "float16"),
+    "RM": ("sbuf", [128, 512], "float16"),
+    "LS": ("sbuf", [128, 192], "uint16"),
+    "cI": ("sbuf", [128, 4], "int32"),
+    "cF": ("sbuf", [128, 4], "float32"),
+    "cA": ("sbuf", [128, 4], "float32"),
+    "tI": ("sbuf", [128, 144], "float32"),
+    "e8": ("sbuf", [128, 128], "float32"),
+    "eB": ("sbuf", [128, 144], "float32"),
+    "kk": ("sbuf", [128, 8], "float32"),
+    "wk": ("sbuf", [128, 8], "float32"),
+    "rv": ("sbuf", [128, 1], "float32"),
+    "R8": ("sbuf", [128, 128], "float16"),
+    "EB": ("sbuf", [128, 144], "bfloat16"),
+    "B": ("sbuf", [128, 144], "float16"),
+    "B1": ("sbuf", [128, 144], "float16"),
+    "BO": ("sbuf", [128, 144], "float16"),
+    "ID": ("sbuf", [128, 128], "float16"),
+    "bw": ("sbuf", [128, 32], "float16"),
+    "key": ("sbuf", [128, 32], "float32"),
+    "keyI": ("sbuf", [128, 32], "int32"),
+    "OI": ("sbuf", [128, 64], "int32"),
+    "OF": ("sbuf", [128, 64], "float32"),
+}
+for _k in range(1, 7):
+    SCRATCH["B2_%d" % _k] = ("sbuf", [128, 144], "bfloat16")
+    SCRATCH["G%d" % _k] = ("sbuf", [128, 512], "bfloat16")
+for _k in range(8):
+    SCRATCH["ps%d" % _k] = ("psum", [128, 512], "float32")
+
+SEMAPHORES = ["lL", "lT", "lK", "aH", "aW", "aI", "sH", "sW", "sI", "oY"] + ["e%d" % k for k in range(100)]
+
+
+def rank_program(g, core, T, topo):
+    rank = T.rank_of(core)
+    if rank is None:
+        return
+    A, ACT = AluOpType, ActivationFunctionType
+    V, S, P, Y = g.vector, g.scalar, g.tensor, g.sync
+    n = len(T.cores)
+    others = [T.cores[(rank + d) % n] for d in range(1, n)]
+    prev = T.cores[(rank - 1) % n]
+    used = [0]
+    evs = []
+
+    def event():
+        e = [T.sem["e%d" % used[0]], 0, 0]
+        used[0] += 1
+        evs.append(e)
+        return e
+
+    def add(e, ins):
+        e[1] += 1
+        ins.then_inc(e[0], 1)
+
+    def one(ins):
+        e = event()
+        add(e, ins)
+        return e
+
+    def wait(q, *es):
+        for e in es:
+            q.wait_ge(e[0], e[1])
+            e[2] = 1
+
+    def send(ap_src, ap_dst, dsts, rsem, lsem):
+        m = topo.mask(core, dsts[0])
+        for d in dsts:
+            m &= topo.mask(core, d)
+        ids = []
+        for d in dsts:
+            a = topo.addr(d)
+            ids.append(DstId(rid=a[0], pnc=a[1]))
+        g.remote_dma_fused([RemoteDMATransfer(dst_ids=ids, dma_engine_mask=m, remote_sem=rsem, srcs=[ap_src],
+                                              dsts=[ap_dst for d in dsts])], local_sem=lsem)
+        return bin(m).count("1")
+
+    w0, w1 = 512 * rank, 512 * rank + 512
+
+    Y.dma_start(T.L8[0:8, :], T.lett[:, :]).then_inc(T.sem.lL, 16)
+    S.dma_start(T.KR[:, 1, :, :], T.kid[1:8:2, :]).then_inc(T.sem.lK, 16)
+    Y.dma_start(T.KR[:, 0, :, :], T.kid[0:8:2, :]).then_inc(T.sem.lK, 16)
+    S.dma_start(T.T8[0:8, :], T.tid[:, :]).then_inc(T.sem.lT, 16)
+
+    c0 = event()
+    add(c0, g.iota(T.cI[:, 0:1], [[0, 1]], 0, 1))
+    add(c0, g.iota(T.e8[0:8, :], [[16, 8], [0, 16]], 0, -16, allow_small_or_imprecise_dtypes=True))
+    c1 = one(g.iota(T.tI[:, :], [[1, 144]], -15, 0, allow_small_or_imprecise_dtypes=True))
+    c2 = event()
+    add(c2, g.iota(T.eB[0:8, :], [[1, 144]], -15, -16, allow_small_or_imprecise_dtypes=True))
+    add(c2, g.iota(T.kk[:, 0:6], [[1, 6]], 1, 0, allow_small_or_imprecise_dtypes=True))
+    wait(V, c0)
+    r8 = one(V.tensor_scalar(T.R8[0:8, :], T.e8[0:8, :], 0.0, None, A.is_equal))
+    v0 = event()
+    add(v0, V.tensor_scalar(T.cI[:, 1:2], T.cI[:, 0:1], 112, None, A.bitwise_and))
+    add(v0, V.tensor_scalar(T.cI[:, 2:3], T.cI[:, 0:1], 15, None, A.bitwise_and))
+    add(v0, V.tensor_scalar(T.cI[:, 3:4], T.cI[:, 0:1], 12, None, A.bitwise_and))
+    wait(V, v0)
+    v1 = one(V.tensor_copy(T.cF[:, :], T.cI[:, :]))
+    wait(V, v1, c1)
+    pcol, s16, ccol, ocol = T.cF[:, 0:1], T.cF[:, 1:2], T.cF[:, 2:3], T.cF[:, 3:4]
+    v2 = event()
+    add(v2, V.tensor_scalar(T.cA[:, 0:1], ccol, 2.0, None, A.is_lt))
+    add(v2, V.tensor_scalar(T.cA[:, 1:2], ccol, 2.0, 65536.0, A.is_equal, A.mult))
+    add(v2, V.tensor_scalar(T.cA[:, 2:3], ocol, 128.0, None, A.mult))
+
+    V.wait_ge(T.sem.lL, 16)
+    lh = one(V.tensor_copy(T.L8h[0:8, :], T.L8[0:8, :]))
+    wait(P, lh, r8)
+    pl = event()
+    for x in range(16):
+        ins = P.matmul(T.ps0[:, x:512:16], T.R8[0:8, :], T.L8h[0:8, 32 * x:32 * x + 32], True, True)
+        if x == 15:
+            add(pl, ins)
+    wait(V, v2)
+    bb = event()
+    add(bb, V.tensor_scalar(T.B[:, :], T.tI[:, :], s16, None, A.is_equal))
+    add(bb, V.tensor_scalar(T.BO[:, :], T.tI[:, :], s16, T.cA[:, 2:3], A.is_equal, A.mult))
+    add(bb, V.tensor_scalar(T.ID[:, :], T.tI[:, 15:143], pcol, None, A.is_equal))
+    wait(V, pl)
+    oh = one(V.tensor_scalar(T.OH[:, 0:512], T.ps0[:, :], ccol, None, A.is_equal))
+    wait(g, oh)
+    nH = send(T.OH[:, 0:80], T.HL[:, :], [prev], T.sem.aH, T.sem.sH)
+
+    V.wait_ge(T.sem.lK, 32)
+    tr = event()
+    for b in range(16):
+        add(tr, V.transpose(T.W[:, w0 + b:w1:16], T.KR[:, :, b, :]))
+    wait(g, tr)
+    nW = send(T.W[:, w0:w1], T.W[:, w0:w1], others, T.sem.aW, T.sem.sW)
+
+    V.wait_ge(T.sem.lT, 16)
+    tf = one(V.tensor_copy(T.T8f[0:8, :], T.T8[0:8, :]))
+    wait(S, tf)
+    hp = one(S.activation(T.H8[0:8, :], T.T8f[0:8, :], ACT.Copy))
+    fp = one(S.activation(T.F8[0:8, :], T.T8f[0:8, :], ACT.Sign))
+    wait(V, c2)
+    eb = one(V.tensor_scalar(T.EB[0:8, :], T.eB[0:8, :], 0.0, None, A.is_equal))
+    wait(V, oh)
+    sh = one(V.tensor_copy(T.OH[:, 512:592], T.OH[:, 1:81]))
+    wk = one(V.tensor_scalar(T.wk[:, 0:6], T.kk[:, 0:6], T.cA[:, 1:2], T.cA[:, 0:1], A.mult, A.add))
+    wait(V, hp, tf)
+    qp = one(V.tensor_tensor(T.Q8[0:8, :], T.T8f[0:8, :], T.H8[0:8, :], A.subtract))
+    wait(P, oh, bb)
+    pb = event()
+    for x in range(16):
+        ins = P.matmul(T.ps2[:, 0:32], T.BO[:, 15 - x:143 - x], T.OH[:, x:512:16], x == 0, x == 15)
+    add(pb, ins)
+    wait(P, eb, hp, fp, qp)
+    P.matmul(T.ps3[:, :], T.EB[0:8, 15:143], T.H8[0:8, :], True, False)
+    P.matmul(T.ps3[:, :], T.EB[0:8, 14:142], T.Q8[0:8, :], False, False)
+    pt = one(P.matmul(T.ps3[:, :], T.EB[0:8, 13:141], T.F8[0:8, :], False, True))
+    wait(S, pt)
+    iw = one(S.activation(T.IDW[:, w0:w1], T.ps3[:, :], ACT.Copy))
+    wait(g, iw)
+    nI = send(T.IDW[:, w0:w1], T.IDW[:, w0:w1], others, T.sem.aI, T.sem.sI)
+    wait(V, wk)
+    b2 = event()
+    for k in range(1, 7):
+        add(b2, V.tensor_scalar(T["B2_%d" % k][:, :], T.tI[:, :], s16, T.wk[:, k - 1:k], A.is_equal, A.mult))
+    wait(V, pb)
+    bw = one(V.tensor_copy(T.bw[:, :], T.ps2[:, 0:32]))
+    wait(V, sh)
+    V.wait_ge(T.sem.aH, nH)
+    hl = one(V.tensor_copy(T.OH[:, 527:592:16], T.HL[:, 0:80:16]))
+
+    V.wait_ge(T.sem.aW, nW * len(others))
+    wait(V, tr)
+    rv = one(V.tensor_reduce(T.rv[:, :], T.W[:, 1:2048:512], AxisListType.X, A.add))
+    wait(V, rv)
+    b1 = one(V.tensor_scalar(T.B1[:, :], T.tI[:, :], s16, T.rv[:, 0:1], A.is_equal, A.mult))
+    wait(V, hl)
+    S.wait_ge(T.sem.aI, nI * len(others))
+    wait(S, iw)
+    pidb = {1: T.ps4, 2: T.ps5, 3: T.ps6, 4: T.ps7, 5: T.ps3, 6: T.ps0}
+
+    def wrap(out, lhs, rhs, first):
+        for x in range(16):
+            ins = P.matmul(out[:, 0:32], lhs[:, 15 - x:143 - x], rhs[:, x:512:16], first and x == 0, x == 15)
+        return one(ins)
+
+    gat, gid, idp, ky = {}, {}, {}, {}
+
+    def keystep(k):
+        wait(V, idp[k])
+        if k == 1:
+            ky[k] = one(V.tensor_copy(T.key[:, :], pidb[k][:, 0:32]))
+        else:
+            wait(V, ky[k - 1])
+            ky[k] = one(V.tensor_tensor(T.key[:, :], T.key[:, :], pidb[k][:, 0:32], A.max))
+
+    wait(P, bw)
+    for k in range(1, 7):
+        ps = T.ps1 if k % 2 else T.ps2
+        P.matmul(ps[:, 0:32], T.ID[:, :], T.bw[:, :], True, False)
+        if k == 1:
+            wait(P, b1)
+            pm = wrap(ps, T.B1, T.OH, False)
+        else:
+            wait(P, gat[k])
+            pm = wrap(ps, T.B, T.RM, False)
+        if k == 2:
+            wait(P, b2)
+        if k > 1:
+            wait(P, gid[k - 1])
+            idp[k - 1] = wrap(pidb[k - 1], T["B2_%d" % (k - 1)], T["G%d" % (k - 1)], True)
+        wait(V, pm)
+        lc = slice(32 * k - 32, 32 * k)
+        ls = one(V.tensor_copy(T.LS[:, lc], ps[:, 0:32]))
+        wait(V, ls)
+        wait(S, ls)
+        if k < 6:
+            gat[k + 1] = one(V.tensor_tensor(T.RM[:, :], T.W[:, :].indirect(T.LS[:, lc]), T.OH[:, 16 * k:16 * k + 512], A.mult))
+            gid[k] = one(S.activation(T["G%d" % k][:, :], T.IDW[:, :].indirect(T.LS[:, lc]), ACT.Copy))
+            if k > 1:
+                keystep(k - 1)
+        else:
+            V.wait_ge(T.sem.aI, nI * len(others))
+            wait(V, iw)
+            ga = one(V.tensor_copy(T.G6[:, 0:256], T.IDW[:, :].indirect(T.LS[:, 160:176])))
+            gb = one(S.activation(T.G6[:, 256:512], T.IDW[:, :].indirect(T.LS[:, 176:192]), ACT.Copy))
+            keystep(5)
+            wait(P, ga, gb)
+            idp[6] = wrap(pidb[6], T.B2_6, T.G6, True)
+    wait(V, idp[6], ky[5])
+    kf = one(V.tensor_tensor(T.keyI[:, :], T.key[:, :], pidb[6][:, 0:32], A.max))
+    wait(V, kf)
+    od = event()
+    add(od, V.tensor_scalar(T.OI[:, 0:32], T.keyI[:, :], 16, None, A.arith_shift_right))
+    add(od, V.tensor_scalar(T.OI[:, 32:64], T.keyI[:, :], 65535, None, A.bitwise_and))
+    wait(V, od)
+    of = one(V.tensor_copy(T.OF[:, :], T.OI[:, :]))
+    wait(Y, of)
+    Y.dma_start(T.ylen[:, :], T.OF[:, 0:32]).then_inc(T.sem.oY, 16)
+    wait(S, of)
+    S.dma_start(T.yid[:, :], T.OF[:, 32:64]).then_inc(T.sem.oY, 16)
+    g.wait_ge(T.sem.sH, nH)
+    g.wait_ge(T.sem.sW, nW)
+    g.wait_ge(T.sem.sI, nI)
+    for e in evs:
+        if not e[2]:
+            wait(g, e)
+    g.wait_ge(T.sem.oY, 32)

@@ -2,7 +2,7 @@ from concourse.bass import DstId, RemoteDMATransfer
 from concourse.mybir import AluOpType, AxisListType, ActivationFunctionType
 
 SCRATCH = {
-    "KR": ("sbuf", [128, 2, 16, 16], "int32"),
+    "KR": ("sbuf", [128, 2, 2, 8, 16], "int32"),
     "W": ("sbuf", [128, 2048], "int32"),
     "IDW": ("sbuf", [128, 2048], "bfloat16"),
     "L8": ("sbuf", [128, 512], "int32"),
@@ -12,8 +12,8 @@ SCRATCH = {
     "H8": ("sbuf", [128, 512], "bfloat16"),
     "F8": ("sbuf", [128, 512], "bfloat16"),
     "Q8": ("sbuf", [128, 512], "bfloat16"),
-    "OH": ("sbuf", [128, 592], "float16"),
-    "HL": ("sbuf", [128, 80], "float16"),
+    "OH": ("sbuf", [128, 520], "float16"),
+    "OHH": ("sbuf", [128, 8], "float16"),
     "RM": ("sbuf", [128, 512], "float16"),
     "LS": ("sbuf", [128, 192], "uint16"),
     "cI": ("sbuf", [128, 4], "int32"),
@@ -32,18 +32,18 @@ SCRATCH = {
     "BO": ("sbuf", [128, 144], "float16"),
     "ID": ("sbuf", [128, 128], "float16"),
     "bw": ("sbuf", [128, 32], "float16"),
-    "key": ("sbuf", [128, 32], "float32"),
-    "keyI": ("sbuf", [128, 32], "int32"),
-    "OI": ("sbuf", [128, 64], "int32"),
-    "OF": ("sbuf", [128, 64], "float32"),
+    "key": ("sbuf", [128, 64], "float32"),
+    "keyI": ("sbuf", [128, 64], "int32"),
+    "OI": ("sbuf", [128, 128], "int32"),
+    "OF": ("sbuf", [128, 128], "float32"),
 }
 for _k in range(1, 7):
-    SCRATCH["B2_%d" % _k] = ("sbuf", [128, 144], "bfloat16")
+    SCRATCH["D%d" % _k] = ("sbuf", [128, 72], "bfloat16")
     SCRATCH["G%d" % _k] = ("sbuf", [128, 512], "bfloat16")
 for _k in range(8):
     SCRATCH["ps%d" % _k] = ("psum", [128, 512], "float32")
 
-SEMAPHORES = ["lL", "lT", "lK", "aH", "aW", "aI", "sH", "sW", "sI", "oY"] + ["e%d" % k for k in range(100)]
+SEMAPHORES = ["lL", "lT", "lK0", "lK1", "aH", "aW0", "aW1", "aI", "sH", "sW0", "sW1", "sI", "oY"] + ["e%d" % k for k in range(100)]
 
 
 def rank_program(g, core, T, topo):
@@ -93,8 +93,10 @@ def rank_program(g, core, T, topo):
     w0, w1 = 512 * rank, 512 * rank + 512
 
     Y.dma_start(T.L8[0:8, :], T.lett[:, :]).then_inc(T.sem.lL, 16)
-    S.dma_start(T.KR[:, 1, :, :], T.kid[1:8:2, :]).then_inc(T.sem.lK, 16)
-    Y.dma_start(T.KR[:, 0, :, :], T.kid[0:8:2, :]).then_inc(T.sem.lK, 16)
+    S.dma_start(T.KR[:, 0, 1, :, :], T.kid[1:8:2, 0:4096]).then_inc(T.sem.lK0, 16)
+    Y.dma_start(T.KR[:, 0, 0, :, :], T.kid[0:8:2, 0:4096]).then_inc(T.sem.lK0, 16)
+    S.dma_start(T.KR[:, 1, 1, :, :], T.kid[1:8:2, 4096:8192]).then_inc(T.sem.lK1, 16)
+    Y.dma_start(T.KR[:, 1, 0, :, :], T.kid[0:8:2, 4096:8192]).then_inc(T.sem.lK1, 16)
     S.dma_start(T.T8[0:8, :], T.tid[:, :]).then_inc(T.sem.lT, 16)
 
     c0 = event()
@@ -118,31 +120,38 @@ def rank_program(g, core, T, topo):
     add(v2, V.tensor_scalar(T.cA[:, 0:1], ccol, 2.0, None, A.is_lt))
     add(v2, V.tensor_scalar(T.cA[:, 1:2], ccol, 2.0, 65536.0, A.is_equal, A.mult))
     add(v2, V.tensor_scalar(T.cA[:, 2:3], ocol, 128.0, None, A.mult))
+    add(v2, V.tensor_scalar(T.cA[:, 3:4], s16, 0.5, None, A.mult))
 
     V.wait_ge(T.sem.lL, 16)
-    lh = one(V.tensor_copy(T.L8h[0:8, :], T.L8[0:8, :]))
+    lh = one(V.tensor_copy(T.L8h[0:8, 0:8], T.L8[0:8, 0:8]))
     wait(P, lh, r8)
-    pl = event()
-    for x in range(16):
-        ins = P.matmul(T.ps0[:, x:512:16], T.R8[0:8, :], T.L8h[0:8, 32 * x:32 * x + 32], True, True)
-        if x == 15:
-            add(pl, ins)
+    ph = one(P.matmul(T.ps1[:, 0:8], T.R8[0:8, :], T.L8h[0:8, 0:8], True, True))
+    wait(V, ph)
+    oh0 = one(V.tensor_scalar(T.OHH[:, :], T.ps1[:, 0:8], ccol, None, A.is_equal))
+    wait(g, oh0)
+    nH = send(T.OHH[:, :], T.OH[:, 512:520], [prev], T.sem.aH, T.sem.sH)
+    lr = one(V.tensor_copy(T.L8h[0:8, 8:512], T.L8[0:8, 8:512]))
+    wait(P, lr)
+    pl = one(P.matmul(T.ps0[:, :], T.R8[0:8, :], T.L8h[0:8, :], True, True))
     wait(V, v2)
     bb = event()
     add(bb, V.tensor_scalar(T.B[:, :], T.tI[:, :], s16, None, A.is_equal))
     add(bb, V.tensor_scalar(T.BO[:, :], T.tI[:, :], s16, T.cA[:, 2:3], A.is_equal, A.mult))
     add(bb, V.tensor_scalar(T.ID[:, :], T.tI[:, 15:143], pcol, None, A.is_equal))
-    wait(V, pl)
-    oh = one(V.tensor_scalar(T.OH[:, 0:512], T.ps0[:, :], ccol, None, A.is_equal))
-    wait(g, oh)
-    nH = send(T.OH[:, 0:80], T.HL[:, :], [prev], T.sem.aH, T.sem.sH)
 
-    V.wait_ge(T.sem.lK, 32)
-    tr = event()
-    for b in range(16):
-        add(tr, V.transpose(T.W[:, w0 + b:w1:16], T.KR[:, :, b, :]))
-    wait(g, tr)
-    nW = send(T.W[:, w0:w1], T.W[:, w0:w1], others, T.sem.aW, T.sem.sW)
+    trs, nW = [], 0
+    for h in range(2):
+        V.wait_ge(T.sem["lK%d" % h], 32)
+        tr = event()
+        a0, a1 = w0 + 256 * h, w0 + 256 * h + 256
+        for b in range(8):
+            add(tr, V.transpose(T.W[:, a0 + b:a1:8], T.KR[:, h, :, b, :]))
+        wait(g, tr)
+        nW = send(T.W[:, a0:a1], T.W[:, a0:a1], others, T.sem["aW%d" % h], T.sem["sW%d" % h])
+        trs.append(tr)
+        if h == 0:
+            wait(V, pl)
+            oh = one(V.tensor_scalar(T.OH[:, 0:512], T.ps0[:, :], ccol, None, A.is_equal))
 
     V.wait_ge(T.sem.lT, 16)
     tf = one(V.tensor_copy(T.T8f[0:8, :], T.T8[0:8, :]))
@@ -151,16 +160,13 @@ def rank_program(g, core, T, topo):
     fp = one(S.activation(T.F8[0:8, :], T.T8f[0:8, :], ACT.Sign))
     wait(V, c2)
     eb = one(V.tensor_scalar(T.EB[0:8, :], T.eB[0:8, :], 0.0, None, A.is_equal))
-    wait(V, oh)
-    sh = one(V.tensor_copy(T.OH[:, 512:592], T.OH[:, 1:81]))
     wk = one(V.tensor_scalar(T.wk[:, 0:6], T.kk[:, 0:6], T.cA[:, 1:2], T.cA[:, 0:1], A.mult, A.add))
     wait(V, hp, tf)
     qp = one(V.tensor_tensor(T.Q8[0:8, :], T.T8f[0:8, :], T.H8[0:8, :], A.subtract))
     wait(P, oh, bb)
-    pb = event()
     for x in range(16):
         ins = P.matmul(T.ps2[:, 0:32], T.BO[:, 15 - x:143 - x], T.OH[:, x:512:16], x == 0, x == 15)
-    add(pb, ins)
+    pb = one(ins)
     wait(P, eb, hp, fp, qp)
     P.matmul(T.ps3[:, :], T.EB[0:8, 15:143], T.H8[0:8, :], True, False)
     P.matmul(T.ps3[:, :], T.EB[0:8, 14:142], T.Q8[0:8, :], False, False)
@@ -172,85 +178,89 @@ def rank_program(g, core, T, topo):
     wait(V, wk)
     b2 = event()
     for k in range(1, 7):
-        add(b2, V.tensor_scalar(T["B2_%d" % k][:, :], T.tI[:, :], s16, T.wk[:, k - 1:k], A.is_equal, A.mult))
+        add(b2, V.tensor_scalar(T["D%d" % k][:, :], T.tI[:, 8:80], T.cA[:, 3:4], T.wk[:, k - 1:k], A.is_equal, A.mult))
     wait(V, pb)
     bw = one(V.tensor_copy(T.bw[:, :], T.ps2[:, 0:32]))
-    wait(V, sh)
-    V.wait_ge(T.sem.aH, nH)
-    hl = one(V.tensor_copy(T.OH[:, 527:592:16], T.HL[:, 0:80:16]))
 
-    V.wait_ge(T.sem.aW, nW * len(others))
-    wait(V, tr)
+    V.wait_ge(T.sem.aW0, nW * len(others))
+    wait(V, trs[0])
     rv = one(V.tensor_reduce(T.rv[:, :], T.W[:, 1:2048:512], AxisListType.X, A.add))
     wait(V, rv)
     b1 = one(V.tensor_scalar(T.B1[:, :], T.tI[:, :], s16, T.rv[:, 0:1], A.is_equal, A.mult))
-    wait(V, hl)
     S.wait_ge(T.sem.aI, nI * len(others))
     wait(S, iw)
-    pidb = {1: T.ps4, 2: T.ps5, 3: T.ps6, 4: T.ps7, 5: T.ps3, 6: T.ps0}
+    bank = {1: T.ps4, 2: T.ps5, 3: T.ps6, 4: T.ps7, 5: T.ps3, 6: T.ps0}
+    gat, gid, idp, ky = {}, {}, {}, {}
 
-    def wrap(out, lhs, rhs, first):
+    def wrap(out, lhs, rhs):
         for x in range(16):
-            ins = P.matmul(out[:, 0:32], lhs[:, 15 - x:143 - x], rhs[:, x:512:16], first and x == 0, x == 15)
+            ins = P.matmul(out[:, 0:32], lhs[:, 15 - x:143 - x], rhs[:, x:512:16], False, x == 15)
         return one(ins)
 
-    gat, gid, idp, ky = {}, {}, {}, {}
+    def idstep(k):
+        wait(P, *gid[k])
+        for b in range(8):
+            ins = P.matmul(bank[k][0:64, 0:64], T["D%d" % k][:, 7 - b:71 - b], T["G%d" % k][:, 64 * b:64 * b + 64], b == 0, b == 7)
+        idp[k] = one(ins)
 
     def keystep(k):
         wait(V, idp[k])
         if k == 1:
-            ky[k] = one(V.tensor_copy(T.key[:, :], pidb[k][:, 0:32]))
+            ky[k] = one(V.tensor_copy(T.key[0:64, :], bank[k][0:64, 0:64]))
         else:
             wait(V, ky[k - 1])
-            ky[k] = one(V.tensor_tensor(T.key[:, :], T.key[:, :], pidb[k][:, 0:32], A.max))
+            ky[k] = one(V.tensor_tensor(T.key[0:64, :], T.key[0:64, :], bank[k][0:64, 0:64], A.max))
 
     wait(P, bw)
+    after = {3: [1], 4: [2, 3], 5: [4], 6: [5]}
     for k in range(1, 7):
         ps = T.ps1 if k % 2 else T.ps2
         P.matmul(ps[:, 0:32], T.ID[:, :], T.bw[:, :], True, False)
         if k == 1:
             wait(P, b1)
-            pm = wrap(ps, T.B1, T.OH, False)
+            pm = wrap(ps, T.B1, T.OH)
         else:
             wait(P, gat[k])
-            pm = wrap(ps, T.B, T.RM, False)
-        if k == 2:
+            pm = wrap(ps, T.B, T.RM)
+        if k == 3:
             wait(P, b2)
-        if k > 1:
-            wait(P, gid[k - 1])
-            idp[k - 1] = wrap(pidb[k - 1], T["B2_%d" % (k - 1)], T["G%d" % (k - 1)], True)
+        for m in after.get(k, []):
+            idstep(m)
         wait(V, pm)
         lc = slice(32 * k - 32, 32 * k)
         ls = one(V.tensor_copy(T.LS[:, lc], ps[:, 0:32]))
+        if k == 1:
+            V.wait_ge(T.sem.aH, nH)
+            V.wait_ge(T.sem.aW1, nW * len(others))
+            wait(V, trs[1])
         wait(V, ls)
         wait(S, ls)
         if k < 6:
-            gat[k + 1] = one(V.tensor_tensor(T.RM[:, :], T.W[:, :].indirect(T.LS[:, lc]), T.OH[:, 16 * k:16 * k + 512], A.mult))
-            gid[k] = one(S.activation(T["G%d" % k][:, :], T.IDW[:, :].indirect(T.LS[:, lc]), ACT.Copy))
-            if k > 1:
-                keystep(k - 1)
+            gat[k + 1] = one(V.tensor_tensor(T.RM[:, :], T.W[:, :].indirect(T.LS[:, lc]), T.OH[:, k:k + 512], A.mult))
+            gid[k] = [one(S.activation(T["G%d" % k][:, :], T.IDW[:, :].indirect(T.LS[:, lc]), ACT.Copy))]
         else:
             V.wait_ge(T.sem.aI, nI * len(others))
             wait(V, iw)
-            ga = one(V.tensor_copy(T.G6[:, 0:256], T.IDW[:, :].indirect(T.LS[:, 160:176])))
-            gb = one(S.activation(T.G6[:, 256:512], T.IDW[:, :].indirect(T.LS[:, 176:192]), ACT.Copy))
-            keystep(5)
-            wait(P, ga, gb)
-            idp[6] = wrap(pidb[6], T.B2_6, T.G6, True)
+            gid[6] = [one(V.tensor_copy(T.G6[:, 0:256], T.IDW[:, :].indirect(T.LS[:, 160:176]))),
+                      one(S.activation(T.G6[:, 256:512], T.IDW[:, :].indirect(T.LS[:, 176:192]), ACT.Copy))]
+            idstep(6)
+        for m in after.get(k, []):
+            keystep(m)
     wait(V, idp[6], ky[5])
-    kf = one(V.tensor_tensor(T.keyI[:, :], T.key[:, :], pidb[6][:, 0:32], A.max))
+    kf = one(V.tensor_tensor(T.keyI[0:64, :], T.key[0:64, :], bank[6][0:64, 0:64], A.max))
     wait(V, kf)
     od = event()
-    add(od, V.tensor_scalar(T.OI[:, 0:32], T.keyI[:, :], 16, None, A.arith_shift_right))
-    add(od, V.tensor_scalar(T.OI[:, 32:64], T.keyI[:, :], 65535, None, A.bitwise_and))
+    add(od, V.tensor_scalar(T.OI[0:64, 0:64], T.keyI[0:64, :], 16, None, A.arith_shift_right))
+    add(od, V.tensor_scalar(T.OI[0:64, 64:128], T.keyI[0:64, :], 65535, None, A.bitwise_and))
     wait(V, od)
-    of = one(V.tensor_copy(T.OF[:, :], T.OI[:, :]))
+    of = one(V.tensor_copy(T.OF[0:64, :], T.OI[0:64, :]))
     wait(Y, of)
-    Y.dma_start(T.ylen[:, :], T.OF[:, 0:32]).then_inc(T.sem.oY, 16)
+    Y.dma_start(T.ylen[:, :], T.OF[0:64, 0:64]).then_inc(T.sem.oY, 16)
     wait(S, of)
-    S.dma_start(T.yid[:, :], T.OF[:, 32:64]).then_inc(T.sem.oY, 16)
+    S.dma_start(T.yid[:, :], T.OF[0:64, 64:128]).then_inc(T.sem.oY, 16)
     g.wait_ge(T.sem.sH, nH)
-    g.wait_ge(T.sem.sW, nW)
+    g.wait_ge(T.sem.sW0, nW)
+    g.wait_ge(T.sem.sW1, nW)
     g.wait_ge(T.sem.sI, nI)
     for e in evs:
         if not e[2]:

@@ -14,7 +14,8 @@ SCRATCH = {
     "Q8": ("sbuf", [128, 512], "bfloat16"),
     "OH": ("sbuf", [128, 520], "float16"),
     "OHH": ("sbuf", [128, 8], "float16"),
-    "RM": ("sbuf", [128, 512], "float16"),
+    "RM0": ("sbuf", [128, 256], "float16"),
+    "RM1": ("sbuf", [128, 256], "float16"),
     "LS": ("sbuf", [128, 192], "uint16"),
     "cI": ("sbuf", [128, 4], "int32"),
     "cF": ("sbuf", [128, 4], "float32"),
@@ -43,7 +44,7 @@ for _k in range(1, 7):
 for _k in range(8):
     SCRATCH["ps%d" % _k] = ("psum", [128, 512], "float32")
 
-SEMAPHORES = ["lL", "lT", "lK0", "lK1", "aH", "aW0", "aW1", "aI", "sH", "sW0", "sW1", "sI", "oY"] + ["e%d" % k for k in range(100)]
+SEMAPHORES = ["lL", "lT", "lK0", "lK1", "aH", "aW0", "aW1", "aI", "sH", "sW0", "sW1", "sI", "oY"] + ["e%d" % k for k in range(120)]
 
 
 def rank_program(g, core, T, topo):
@@ -190,18 +191,15 @@ def rank_program(g, core, T, topo):
     S.wait_ge(T.sem.aI, nI * len(others))
     wait(S, iw)
     bank = {1: T.ps4, 2: T.ps5, 3: T.ps6, 4: T.ps7, 5: T.ps3, 6: T.ps0}
+    acc = [T.ps1, T.ps2]
     gat, gid, idp, ky = {}, {}, {}, {}
 
-    def wrap(out, lhs, rhs):
-        for x in range(16):
-            ins = P.matmul(out[:, 0:32], lhs[:, 15 - x:143 - x], rhs[:, x:512:16], False, x == 15)
-        return one(ins)
-
-    def idstep(k):
-        wait(P, *gid[k])
-        for b in range(8):
+    def idstep(k, bs, es):
+        wait(P, *es)
+        for b in bs:
             ins = P.matmul(bank[k][0:64, 0:64], T["D%d" % k][:, 7 - b:71 - b], T["G%d" % k][:, 64 * b:64 * b + 64], b == 0, b == 7)
-        idp[k] = one(ins)
+        if b == 7:
+            idp[k] = one(ins)
 
     def keystep(k):
         wait(V, idp[k])
@@ -211,39 +209,50 @@ def rank_program(g, core, T, topo):
             wait(V, ky[k - 1])
             ky[k] = one(V.tensor_tensor(T.key[0:64, :], T.key[0:64, :], bank[k][0:64, 0:64], A.max))
 
-    wait(P, bw)
-    after = {3: [1], 4: [2, 3], 5: [4], 6: [5]}
+    wait(P, bw, b1)
+    after = {4: [1, 2], 5: [3, 4], 6: [5]}
     for k in range(1, 7):
-        ps = T.ps1 if k % 2 else T.ps2
-        P.matmul(ps[:, 0:32], T.ID[:, :], T.bw[:, :], True, False)
-        if k == 1:
-            wait(P, b1)
-            pm = wrap(ps, T.B1, T.OH)
-        else:
-            wait(P, gat[k])
-            pm = wrap(ps, T.B, T.RM)
-        if k == 3:
+        pm = []
+        for s in range(2):
+            if k > 1:
+                wait(P, gat[k, s])
+            P.matmul(acc[s][:, 0:16], T.ID[:, :], T.bw[:, 16 * s:16 * s + 16], True, False)
+            for x in range(16):
+                if k == 1:
+                    ins = P.matmul(acc[s][:, 0:16], T.B1[:, 15 - x:143 - x], T.OH[:, 256 * s + x:256 * s + 256:16], False, x == 15)
+                else:
+                    ins = P.matmul(acc[s][:, 0:16], T.B[:, 15 - x:143 - x], T["RM%d" % s][:, x:256:16], False, x == 15)
+            pm.append(one(ins))
+        if k == 4:
             wait(P, b2)
         for m in after.get(k, []):
-            idstep(m)
-        wait(V, pm)
-        lc = slice(32 * k - 32, 32 * k)
-        ls = one(V.tensor_copy(T.LS[:, lc], ps[:, 0:32]))
-        if k == 1:
-            V.wait_ge(T.sem.aH, nH)
-            V.wait_ge(T.sem.aW1, nW * len(others))
-            wait(V, trs[1])
-        wait(V, ls)
-        wait(S, ls)
+            idstep(m, range(8), [gid[m]])
+        ls = []
+        for s in range(2):
+            c = 32 * k - 32 + 16 * s
+            wait(V, pm[s])
+            ls.append(one(V.tensor_copy(T.LS[:, c:c + 16], acc[s][:, 0:16])))
+            if k == 1 and s == 0:
+                V.wait_ge(T.sem.aH, nH)
+                V.wait_ge(T.sem.aW1, nW * len(others))
+                wait(V, trs[1])
+            wait(V, ls[s])
+            if k < 6:
+                gat[k + 1, s] = one(V.tensor_tensor(T["RM%d" % s][:, :], T.W[:, :].indirect(T.LS[:, c:c + 16]),
+                                                    T.OH[:, 256 * s + k:256 * s + k + 256], A.mult))
+            elif s == 0:
+                V.wait_ge(T.sem.aI, nI * len(others))
+                wait(V, iw)
+                i0 = one(V.tensor_copy(T.G6[:, 0:256], T.IDW[:, :].indirect(T.LS[:, c:c + 16])))
+                idstep(6, range(4), [i0])
+            else:
+                wait(S, ls[1])
+                i1 = one(V.tensor_copy(T.G6[:, 256:384], T.IDW[:, :].indirect(T.LS[:, c:c + 8])))
+                i2 = one(S.activation(T.G6[:, 384:512], T.IDW[:, :].indirect(T.LS[:, c + 8:c + 16]), ACT.Copy))
+                idstep(6, range(4, 8), [i1, i2])
         if k < 6:
-            gat[k + 1] = one(V.tensor_tensor(T.RM[:, :], T.W[:, :].indirect(T.LS[:, lc]), T.OH[:, k:k + 512], A.mult))
-            gid[k] = [one(S.activation(T["G%d" % k][:, :], T.IDW[:, :].indirect(T.LS[:, lc]), ACT.Copy))]
-        else:
-            V.wait_ge(T.sem.aI, nI * len(others))
-            wait(V, iw)
-            gid[6] = [one(V.tensor_copy(T.G6[:, 0:256], T.IDW[:, :].indirect(T.LS[:, 160:176]))),
-                      one(S.activation(T.G6[:, 256:512], T.IDW[:, :].indirect(T.LS[:, 176:192]), ACT.Copy))]
-            idstep(6)
+            wait(S, ls[0], ls[1])
+            gid[k] = one(S.activation(T["G%d" % k][:, :], T.IDW[:, :].indirect(T.LS[:, 32 * k - 32:32 * k]), ACT.Copy))
         for m in after.get(k, []):
             keystep(m)
     wait(V, idp[6], ky[5])

@@ -1,38 +1,48 @@
 from concourse.bass import DstId, RemoteDMATransfer
 from concourse.mybir import AluOpType, AxisListType, ActivationFunctionType
 
+NB = [6, 10]
+
 SCRATCH = {
-    "KR": ("sbuf", [128, 2, 2, 8, 16], "int32"),
-    "W": ("sbuf", [128, 2048], "int32"),
+    "KR0": ("sbuf", [128, 2, NB[0], 16], "int32"),
+    "KR1": ("sbuf", [128, 2, NB[1], 16], "int32"),
+    "KB0": ("sbuf", [128, 2, NB[0], 16], "bfloat16"),
+    "KB1": ("sbuf", [128, 2, NB[1], 16], "bfloat16"),
+    "W": ("sbuf", [128, 2048], "bfloat16"),
     "IDW": ("sbuf", [128, 2048], "bfloat16"),
-    "L8": ("sbuf", [128, 512], "int32"),
-    "L8h": ("sbuf", [128, 512], "float16"),
-    "T8": ("sbuf", [128, 512], "int32"),
-    "T8f": ("sbuf", [128, 512], "float32"),
-    "H8": ("sbuf", [128, 512], "bfloat16"),
-    "F8": ("sbuf", [128, 512], "bfloat16"),
-    "Q8": ("sbuf", [128, 512], "bfloat16"),
+    "Lw": ("sbuf", [128, 32], "int32"),
+    "Ln": ("sbuf", [128, 32], "int32"),
+    "Lnh": ("sbuf", [128, 8], "float16"),
+    "L4": ("sbuf", [128, 128], "int32"),
+    "L4h": ("sbuf", [128, 128], "bfloat16"),
+    "T4": ("sbuf", [128, 128], "int32"),
+    "T4f": ("sbuf", [128, 128], "float32"),
+    "X4": ("sbuf", [128, 128], "bfloat16"),
     "OH": ("sbuf", [128, 520], "float16"),
-    "OHH": ("sbuf", [128, 8], "float16"),
     "RM0": ("sbuf", [128, 256], "float16"),
     "RM1": ("sbuf", [128, 256], "float16"),
     "LS": ("sbuf", [128, 192], "uint16"),
     "cI": ("sbuf", [128, 4], "int32"),
     "cF": ("sbuf", [128, 4], "float32"),
-    "cA": ("sbuf", [128, 4], "float32"),
+    "cA": ("sbuf", [128, 8], "float32"),
     "tI": ("sbuf", [128, 144], "float32"),
-    "e8": ("sbuf", [128, 128], "float32"),
-    "eB": ("sbuf", [128, 144], "float32"),
+    "eR": ("sbuf", [128, 128], "float32"),
+    "eE": ("sbuf", [128, 128], "float32"),
+    "eG": ("sbuf", [128, 128], "float32"),
+    "aR": ("sbuf", [128, 512], "float32"),
+    "aE": ("sbuf", [128, 512], "float32"),
+    "RQ": ("sbuf", [128, 512], "bfloat16"),
+    "EQ": ("sbuf", [128, 512], "bfloat16"),
     "kk": ("sbuf", [128, 8], "float32"),
     "wk": ("sbuf", [128, 8], "float32"),
     "rv": ("sbuf", [128, 1], "float32"),
-    "R8": ("sbuf", [128, 128], "float16"),
-    "EB": ("sbuf", [128, 144], "bfloat16"),
+    "RG": ("sbuf", [128, 128], "float16"),
     "B": ("sbuf", [128, 144], "float16"),
     "B1": ("sbuf", [128, 144], "float16"),
     "BO": ("sbuf", [128, 144], "float16"),
     "ID": ("sbuf", [128, 128], "float16"),
     "bw": ("sbuf", [128, 32], "float16"),
+    "bw1": ("sbuf", [128, 32], "float16"),
     "key": ("sbuf", [128, 64], "float32"),
     "keyI": ("sbuf", [128, 64], "int32"),
     "OI": ("sbuf", [128, 128], "int32"),
@@ -44,7 +54,7 @@ for _k in range(1, 7):
 for _k in range(8):
     SCRATCH["ps%d" % _k] = ("psum", [128, 512], "float32")
 
-SEMAPHORES = ["lL", "lT", "lK0", "lK1", "aH", "aW0", "aW1", "aI", "sH", "sW0", "sW1", "sI", "oY"] + ["e%d" % k for k in range(120)]
+SEMAPHORES = ["lL", "lw", "lT", "lK0", "lK1", "aH", "aW0", "aW1", "aI", "sH", "sW0", "sW1", "sI", "oY"] + ["e%d" % k for k in range(130)]
 
 
 def rank_program(g, core, T, topo):
@@ -92,96 +102,120 @@ def rank_program(g, core, T, topo):
         return bin(m).count("1")
 
     w0, w1 = 512 * rank, 512 * rank + 512
+    at = [0, 32 * NB[0], 512]
 
-    Y.dma_start(T.L8[0:8, :], T.lett[:, :]).then_inc(T.sem.lL, 16)
-    S.dma_start(T.KR[:, 0, 1, :, :], T.kid[1:8:2, 0:4096]).then_inc(T.sem.lK0, 16)
-    Y.dma_start(T.KR[:, 0, 0, :, :], T.kid[0:8:2, 0:4096]).then_inc(T.sem.lK0, 16)
-    S.dma_start(T.KR[:, 1, 1, :, :], T.kid[1:8:2, 4096:8192]).then_inc(T.sem.lK1, 16)
-    Y.dma_start(T.KR[:, 1, 0, :, :], T.kid[0:8:2, 4096:8192]).then_inc(T.sem.lK1, 16)
-    S.dma_start(T.T8[0:8, :], T.tid[:, :]).then_inc(T.sem.lT, 16)
+    def kid(q, h, g2):
+        q.dma_start(T["KR%d" % h][:, g2, :, :], T.kid[g2:8:2, 16 * at[h]:16 * at[h + 1]]).then_inc(T.sem["lK%d" % h], 16)
 
+    Y.dma_start(T.Lw[:, :], T.lett[:, :]).then_inc(T.sem.lw, 16)
+    kid(S, 0, 1)
+    kid(Y, 0, 0)
+    S.dma_start(T.L4[0:32, :], T.lett[:, :]).then_inc(T.sem.lL, 16)
+    kid(Y, 1, 0)
+    kid(S, 1, 1)
+    S.dma_start(T.T4[0:32, :], T.tid[:, :]).then_inc(T.sem.lT, 16)
+    Y.dma_start(T.T4[32:64, :], T.tid[:, :]).then_inc(T.sem.lT, 16)
+    Y.dma_start(T.T4[64:96, :], T.tid[:, :]).then_inc(T.sem.lT, 16)
+
+    imp = {"allow_small_or_imprecise_dtypes": True}
     c0 = event()
     add(c0, g.iota(T.cI[:, 0:1], [[0, 1]], 0, 1))
-    add(c0, g.iota(T.e8[0:8, :], [[16, 8], [0, 16]], 0, -16, allow_small_or_imprecise_dtypes=True))
-    c1 = one(g.iota(T.tI[:, :], [[1, 144]], -15, 0, allow_small_or_imprecise_dtypes=True))
-    c2 = event()
-    add(c2, g.iota(T.eB[0:8, :], [[1, 144]], -15, -16, allow_small_or_imprecise_dtypes=True))
-    add(c2, g.iota(T.kk[:, 0:6], [[1, 6]], 1, 0, allow_small_or_imprecise_dtypes=True))
+    add(c0, g.iota(T.kk[:, 0:6], [[1, 6]], 1, 0, **imp))
+    c1 = one(g.iota(T.tI[:, :], [[1, 144]], -15, 0, **imp))
+    c2 = one(g.iota(T.eR[0:32, :], [[4, 8], [0, 16]], 0, -1, **imp))
+    c3 = one(g.iota(T.eE[0:96, :], [[4, 8], [32, 16]], 0, -1, **imp))
+    c4 = one(g.iota(T.eG[:, :], [[16, 8], [0, 16]], 0, -1, **imp))
+    g.wait_ge(T.sem.lw, 16)
+    nH = send(T.Lw[:, :], T.Ln[:, :], [prev], T.sem.aH, T.sem.sH)
+    wait(S, c0)
+    sel = []
+    for c, e, a, o, p in ((c2, T.eR, T.aR, T.RQ, 32), (c3, T.eE, T.aE, T.EQ, 96)):
+        wait(S, c)
+        ab = event()
+        add(ab, S.activation(a[0:p, 0:128], e[0:p, :], ACT.Abs))
+        for q in range(1, 4):
+            add(ab, S.activation(a[0:p, 128 * q:128 * q + 128], e[0:p, :], ACT.Abs, bias=T.kk[0:p, q - 1:q]))
+        wait(S, ab)
+        sel.append(one(S.activation(o[0:p, :], a[0:p, :], ACT.Relu, scale=-1.0, bias=T.kk[0:p, 0:1])))
     wait(V, c0)
-    r8 = one(V.tensor_scalar(T.R8[0:8, :], T.e8[0:8, :], 0.0, None, A.is_equal))
     v0 = event()
     add(v0, V.tensor_scalar(T.cI[:, 1:2], T.cI[:, 0:1], 112, None, A.bitwise_and))
     add(v0, V.tensor_scalar(T.cI[:, 2:3], T.cI[:, 0:1], 15, None, A.bitwise_and))
     add(v0, V.tensor_scalar(T.cI[:, 3:4], T.cI[:, 0:1], 12, None, A.bitwise_and))
     wait(V, v0)
     v1 = one(V.tensor_copy(T.cF[:, :], T.cI[:, :]))
-    wait(V, v1, c1)
+    wait(V, v1)
     pcol, s16, ccol, ocol = T.cF[:, 0:1], T.cF[:, 1:2], T.cF[:, 2:3], T.cF[:, 3:4]
     v2 = event()
     add(v2, V.tensor_scalar(T.cA[:, 0:1], ccol, 2.0, None, A.is_lt))
     add(v2, V.tensor_scalar(T.cA[:, 1:2], ccol, 2.0, 65536.0, A.is_equal, A.mult))
     add(v2, V.tensor_scalar(T.cA[:, 2:3], ocol, 128.0, None, A.mult))
     add(v2, V.tensor_scalar(T.cA[:, 3:4], s16, 0.5, None, A.mult))
-
-    V.wait_ge(T.sem.lL, 16)
-    lh = one(V.tensor_copy(T.L8h[0:8, 0:8], T.L8[0:8, 0:8]))
-    wait(P, lh, r8)
-    ph = one(P.matmul(T.ps1[:, 0:8], T.R8[0:8, :], T.L8h[0:8, 0:8], True, True))
-    wait(V, ph)
-    oh0 = one(V.tensor_scalar(T.OHH[:, :], T.ps1[:, 0:8], ccol, None, A.is_equal))
-    wait(g, oh0)
-    nH = send(T.OHH[:, :], T.OH[:, 512:520], [prev], T.sem.aH, T.sem.sH)
-    lr = one(V.tensor_copy(T.L8h[0:8, 8:512], T.L8[0:8, 8:512]))
-    wait(P, lr)
-    pl = one(P.matmul(T.ps0[:, :], T.R8[0:8, :], T.L8h[0:8, :], True, True))
-    wait(V, v2)
-    bb = event()
-    add(bb, V.tensor_scalar(T.B[:, :], T.tI[:, :], s16, None, A.is_equal))
-    add(bb, V.tensor_scalar(T.BO[:, :], T.tI[:, :], s16, T.cA[:, 2:3], A.is_equal, A.mult))
-    add(bb, V.tensor_scalar(T.ID[:, :], T.tI[:, 15:143], pcol, None, A.is_equal))
-
-    trs, nW = [], 0
-    for h in range(2):
-        V.wait_ge(T.sem["lK%d" % h], 32)
-        tr = event()
-        a0, a1 = w0 + 256 * h, w0 + 256 * h + 256
-        for b in range(8):
-            add(tr, V.transpose(T.W[:, a0 + b:a1:8], T.KR[:, h, :, b, :]))
-        wait(g, tr)
-        nW = send(T.W[:, a0:a1], T.W[:, a0:a1], others, T.sem["aW%d" % h], T.sem["sW%d" % h])
-        trs.append(tr)
-        if h == 0:
-            wait(V, pl)
-            oh = one(V.tensor_scalar(T.OH[:, 0:512], T.ps0[:, :], ccol, None, A.is_equal))
-
-    V.wait_ge(T.sem.lT, 16)
-    tf = one(V.tensor_copy(T.T8f[0:8, :], T.T8[0:8, :]))
-    wait(S, tf)
-    hp = one(S.activation(T.H8[0:8, :], T.T8f[0:8, :], ACT.Copy))
-    fp = one(S.activation(T.F8[0:8, :], T.T8f[0:8, :], ACT.Sign))
-    wait(V, c2)
-    eb = one(V.tensor_scalar(T.EB[0:8, :], T.eB[0:8, :], 0.0, None, A.is_equal))
+    wait(V, v2, c1)
     wk = one(V.tensor_scalar(T.wk[:, 0:6], T.kk[:, 0:6], T.cA[:, 1:2], T.cA[:, 0:1], A.mult, A.add))
-    wait(V, hp, tf)
-    qp = one(V.tensor_tensor(T.Q8[0:8, :], T.T8f[0:8, :], T.H8[0:8, :], A.subtract))
-    wait(P, oh, bb)
-    for x in range(16):
-        ins = P.matmul(T.ps2[:, 0:32], T.BO[:, 15 - x:143 - x], T.OH[:, x:512:16], x == 0, x == 15)
-    pb = one(ins)
-    wait(P, eb, hp, fp, qp)
-    P.matmul(T.ps3[:, :], T.EB[0:8, 15:143], T.H8[0:8, :], True, False)
-    P.matmul(T.ps3[:, :], T.EB[0:8, 14:142], T.Q8[0:8, :], False, False)
-    pt = one(P.matmul(T.ps3[:, :], T.EB[0:8, 13:141], T.F8[0:8, :], False, True))
-    wait(S, pt)
-    iw = one(S.activation(T.IDW[:, w0:w1], T.ps3[:, :], ACT.Copy))
-    wait(g, iw)
-    nI = send(T.IDW[:, w0:w1], T.IDW[:, w0:w1], others, T.sem.aI, T.sem.sI)
+    bb = event()
+    add(bb, V.tensor_scalar(T.BO[:, :], T.tI[:, :], s16, T.cA[:, 2:3], A.is_equal, A.mult))
+    add(bb, V.tensor_scalar(T.B[:, :], T.tI[:, :], s16, None, A.is_equal))
+    add(bb, V.tensor_scalar(T.ID[:, :], T.tI[:, 15:143], pcol, None, A.is_equal))
     wait(V, wk)
     b2 = event()
     for k in range(1, 7):
         add(b2, V.tensor_scalar(T["D%d" % k][:, :], T.tI[:, 8:80], T.cA[:, 3:4], T.wk[:, k - 1:k], A.is_equal, A.mult))
+    wait(V, c4)
+    rg = one(V.tensor_scalar(T.RG[:, :], T.eG[:, :], 0.0, None, A.is_equal))
+
+    V.wait_ge(T.sem.lL, 16)
+    lr = one(V.tensor_copy(T.L4h[0:32, :], T.L4[0:32, :]))
+    wait(P, lr, sel[0])
+    for q in range(4):
+        ins = P.matmul(T.ps0[:, 128 * q:128 * q + 128], T.RQ[0:32, 128 * q:128 * q + 128], T.L4h[0:32, :], True, True)
+    pl = one(ins)
+
+    trs, nW = [], 0
+    for h in range(2):
+        kr, kb, nb = T["KR%d" % h], T["KB%d" % h], NB[h]
+        V.wait_ge(T.sem["lK%d" % h], 32)
+        cv = [one(V.tensor_scalar(kb[:, :, u:u + nb // 2, :], kr[:, :, u:u + nb // 2, :], -256.0, None, A.add)) for u in (0, nb // 2)]
+        tr = event()
+        a0, a1 = w0 + at[h], w0 + at[h + 1]
+        for b in range(nb):
+            if b % (nb // 2) == 0:
+                wait(V, cv[b // (nb // 2)])
+            add(tr, V.transpose(T.W[:, a0 + b:a1:nb], kb[:, :, b, :]))
+        wait(g, tr)
+        nW = send(T.W[:, a0:a1], T.W[:, a0:a1], others, T.sem["aW%d" % h], T.sem["sW%d" % h])
+        trs.append(tr)
+
+    V.wait_ge(T.sem.lT, 48)
+    tf = one(V.tensor_copy(T.T4f[0:96, :], T.T4[0:96, :]))
+    wait(S, tf)
+    hp = one(S.activation(T.X4[0:64, :], T.T4f[0:64, :], ACT.Copy))
+    fp = one(S.activation(T.X4[64:96, :], T.T4f[64:96, :], ACT.Sign))
+    wait(V, pl)
+    oh = one(V.tensor_scalar(T.OH[:, 0:512], T.ps0[:, :], ccol, None, A.is_equal))
+    wait(V, hp, tf)
+    qp = one(V.tensor_tensor(T.X4[32:64, :], T.T4f[32:64, :], T.X4[32:64, :], A.subtract))
+    wait(P, sel[1], hp, fp, qp)
+    for q in range(4):
+        ins = P.matmul(T.ps3[:, 128 * q:128 * q + 128], T.EQ[0:96, 128 * q:128 * q + 128], T.X4[0:96, :], True, True)
+    pt = one(ins)
+    wait(P, oh, bb)
+    for x in range(16):
+        ins = P.matmul(T.ps2[:, 0:32], T.BO[:, 15 - x:143 - x], T.OH[:, x:512:16], x == 0, x == 15)
+    pb = one(ins)
+    wait(S, pt)
+    iw = one(S.activation(T.IDW[:, w0:w1], T.ps3[:, :], ACT.Copy))
+    wait(g, iw)
+    nI = send(T.IDW[:, w0:w1], T.IDW[:, w0:w1], others, T.sem.aI, T.sem.sI)
+    V.wait_ge(T.sem.aH, nH)
+    ln = one(V.tensor_copy(T.Lnh[:, :], T.Ln[:, 0:8]))
+    wait(P, ln, rg)
+    ph = one(P.matmul(T.ps4[:, 0:8], T.RG[:, :], T.Lnh[:, :], True, True))
     wait(V, pb)
-    bw = one(V.tensor_copy(T.bw[:, :], T.ps2[:, 0:32]))
+    bw1 = one(V.tensor_scalar(T.bw1[:, :], T.ps2[:, 0:32], 1024.0, None, A.add))
+    bw = one(V.tensor_scalar(T.bw[:, :], T.ps2[:, 0:32], 256.0, None, A.add))
+    wait(V, ph)
+    ohn = one(V.tensor_scalar(T.OH[:, 512:520], T.ps4[:, 0:8], ccol, None, A.is_equal))
 
     V.wait_ge(T.sem.aW0, nW * len(others))
     wait(V, trs[0])
@@ -192,7 +226,7 @@ def rank_program(g, core, T, topo):
     wait(S, iw)
     bank = {1: T.ps4, 2: T.ps5, 3: T.ps6, 4: T.ps7, 5: T.ps3, 6: T.ps0}
     acc = [T.ps1, T.ps2]
-    gat, gid, idp, ky = {}, {}, {}, {}
+    gat, gid, idp, ky, ls = {}, {}, {}, {}, {}
 
     def idstep(k, bs, es):
         wait(P, *es)
@@ -209,14 +243,16 @@ def rank_program(g, core, T, topo):
             wait(V, ky[k - 1])
             ky[k] = one(V.tensor_tensor(T.key[0:64, :], T.key[0:64, :], bank[k][0:64, 0:64], A.max))
 
-    wait(P, bw, b1)
-    after = {4: [1, 2], 5: [3, 4], 6: [5]}
+    wait(P, bw1, bw, ohn)
+    ids = {4: [1], 5: [2, 3], 6: [4, 5]}
+    keys = {(5, 0): [1], (6, 0): [2], (6, 1): [3]}
     for k in range(1, 7):
         pm = []
         for s in range(2):
             if k > 1:
-                wait(P, gat[k, s])
-            P.matmul(acc[s][:, 0:16], T.ID[:, :], T.bw[:, 16 * s:16 * s + 16], True, False)
+                wait(P, ls[k - 1, s])
+            P.matmul(acc[s][:, 0:16], T.ID[:, :], (T.bw1 if k == 1 else T.bw)[:, 16 * s:16 * s + 16], True, False)
+            wait(P, b1 if k == 1 else gat[k, s])
             for x in range(16):
                 if k == 1:
                     ins = P.matmul(acc[s][:, 0:16], T.B1[:, 15 - x:143 - x], T.OH[:, 256 * s + x:256 * s + 256:16], False, x == 15)
@@ -225,18 +261,18 @@ def rank_program(g, core, T, topo):
             pm.append(one(ins))
         if k == 4:
             wait(P, b2)
-        for m in after.get(k, []):
+        for m in ids.get(k, []):
             idstep(m, range(8), [gid[m]])
-        ls = []
         for s in range(2):
             c = 32 * k - 32 + 16 * s
             wait(V, pm[s])
-            ls.append(one(V.tensor_copy(T.LS[:, c:c + 16], acc[s][:, 0:16])))
+            ls[k, s] = one(V.tensor_copy(T.LS[:, c:c + 16], acc[s][:, 0:16]))
+            for m in keys.get((k, s), []):
+                keystep(m)
             if k == 1 and s == 0:
-                V.wait_ge(T.sem.aH, nH)
+                wait(V, ohn, trs[1])
                 V.wait_ge(T.sem.aW1, nW * len(others))
-                wait(V, trs[1])
-            wait(V, ls[s])
+            wait(V, ls[k, s])
             if k < 6:
                 gat[k + 1, s] = one(V.tensor_tensor(T["RM%d" % s][:, :], T.W[:, :].indirect(T.LS[:, c:c + 16]),
                                                     T.OH[:, 256 * s + k:256 * s + k + 256], A.mult))
@@ -246,15 +282,15 @@ def rank_program(g, core, T, topo):
                 i0 = one(V.tensor_copy(T.G6[:, 0:256], T.IDW[:, :].indirect(T.LS[:, c:c + 16])))
                 idstep(6, range(4), [i0])
             else:
-                wait(S, ls[1])
+                wait(S, ls[k, 1])
                 i1 = one(V.tensor_copy(T.G6[:, 256:384], T.IDW[:, :].indirect(T.LS[:, c:c + 8])))
                 i2 = one(S.activation(T.G6[:, 384:512], T.IDW[:, :].indirect(T.LS[:, c + 8:c + 16]), ACT.Copy))
                 idstep(6, range(4, 8), [i1, i2])
         if k < 6:
-            wait(S, ls[0], ls[1])
+            wait(S, ls[k, 0], ls[k, 1])
             gid[k] = one(S.activation(T["G%d" % k][:, :], T.IDW[:, :].indirect(T.LS[:, 32 * k - 32:32 * k]), ACT.Copy))
-        for m in after.get(k, []):
-            keystep(m)
+    keystep(4)
+    keystep(5)
     wait(V, idp[6], ky[5])
     kf = one(V.tensor_tensor(T.keyI[0:64, :], T.key[0:64, :], bank[6][0:64, 0:64], A.max))
     wait(V, kf)

@@ -1,17 +1,17 @@
 from concourse.bass import DstId, RemoteDMATransfer
 from concourse.mybir import AluOpType, AxisListType, ActivationFunctionType
 
-NB = [6, 10]
+R = 8
 
 SCRATCH = {
-    "KR0": ("sbuf", [128, 2, NB[0], 16], "int32"),
-    "KR1": ("sbuf", [128, 2, NB[1], 16], "int32"),
-    "KB0": ("sbuf", [128, 2, NB[0], 16], "bfloat16"),
-    "KB1": ("sbuf", [128, 2, NB[1], 16], "bfloat16"),
+    "KR": ("sbuf", [128, 4, R, 16], "int32"),
+    "KB": ("sbuf", [128, 2, R, 32], "bfloat16"),
+    "I4": ("sbuf", [128, 32], "bfloat16"),
     "W": ("sbuf", [128, 2048], "bfloat16"),
     "IDW": ("sbuf", [128, 2048], "bfloat16"),
-    "Lw": ("sbuf", [128, 32], "int32"),
-    "Ln": ("sbuf", [128, 32], "int32"),
+    "RS": ("sbuf", [128, 144], "int32"),
+    "r2": ("sbuf", [128, 2], "float32"),
+    "rv": ("sbuf", [128, 1], "float32"),
     "Lnh": ("sbuf", [128, 8], "float16"),
     "L4": ("sbuf", [128, 128], "int32"),
     "L4h": ("sbuf", [128, 128], "bfloat16"),
@@ -22,39 +22,44 @@ SCRATCH = {
     "RM0": ("sbuf", [128, 256], "float16"),
     "RM1": ("sbuf", [128, 256], "float16"),
     "LS": ("sbuf", [128, 192], "uint16"),
-    "cI": ("sbuf", [128, 4], "int32"),
-    "cF": ("sbuf", [128, 4], "float32"),
+    "cI": ("sbuf", [128, 5], "int32"),
+    "cF": ("sbuf", [128, 5], "float32"),
     "cA": ("sbuf", [128, 8], "float32"),
-    "tI": ("sbuf", [128, 144], "float32"),
+    "tI": ("sbuf", [128, 144], "bfloat16"),
+    "tD": ("sbuf", [128, 136], "float32"),
+    "pA": ("sbuf", [128, 136], "float32"),
+    "pP": ("sbuf", [128, 136], "float32"),
     "eR": ("sbuf", [128, 128], "float32"),
     "eE": ("sbuf", [128, 128], "float32"),
-    "eG": ("sbuf", [128, 128], "float32"),
+    "eG": ("sbuf", [128, 128], "bfloat16"),
     "aR": ("sbuf", [128, 512], "float32"),
     "aE": ("sbuf", [128, 512], "float32"),
     "RQ": ("sbuf", [128, 512], "bfloat16"),
     "EQ": ("sbuf", [128, 512], "bfloat16"),
-    "kk": ("sbuf", [128, 8], "float32"),
+    "kk": ("sbuf", [128, 32], "float32"),
     "wk": ("sbuf", [128, 8], "float32"),
-    "rv": ("sbuf", [128, 1], "float32"),
     "RG": ("sbuf", [128, 128], "float16"),
     "B": ("sbuf", [128, 144], "float16"),
     "B1": ("sbuf", [128, 144], "float16"),
     "BO": ("sbuf", [128, 144], "float16"),
-    "ID": ("sbuf", [128, 128], "float16"),
-    "bw": ("sbuf", [128, 32], "float16"),
-    "bw1": ("sbuf", [128, 32], "float16"),
+    "ID": ("sbuf", [128, 128], "bfloat16"),
+    "bw": ("sbuf", [128, 32], "bfloat16"),
+    "DI": ("sbuf", [128, 72], "bfloat16"),
     "key": ("sbuf", [128, 64], "float32"),
     "keyI": ("sbuf", [128, 64], "int32"),
-    "OI": ("sbuf", [128, 128], "int32"),
-    "OF": ("sbuf", [128, 128], "float32"),
+    "idI": ("sbuf", [128, 64], "int32"),
+    "kI": ("sbuf", [128, 64], "int32"),
+    "u": ("sbuf", [128, 64], "float32"),
+    "OL": ("sbuf", [128, 64], "float32"),
+    "OD": ("sbuf", [128, 64], "float32"),
 }
 for _k in range(1, 7):
-    SCRATCH["D%d" % _k] = ("sbuf", [128, 72], "bfloat16")
+    SCRATCH["D%d" % _k] = ("sbuf", [128, 136], "bfloat16")
     SCRATCH["G%d" % _k] = ("sbuf", [128, 512], "bfloat16")
 for _k in range(8):
     SCRATCH["ps%d" % _k] = ("psum", [128, 512], "float32")
 
-SEMAPHORES = ["lL", "lw", "lT", "lK0", "lK1", "aH", "aW0", "aW1", "aI", "sH", "sW0", "sW1", "sI", "oY"] + ["e%d" % k for k in range(130)]
+SEMAPHORES = ["lL", "lR", "lT", "lK0", "lK1", "lK2", "lK3", "aH", "aW0", "aW1", "aI", "sH", "sW0", "sW1", "sI", "oY"] + ["e%d" % k for k in range(134)]
 
 
 def rank_program(g, core, T, topo):
@@ -65,7 +70,6 @@ def rank_program(g, core, T, topo):
     V, S, P, Y = g.vector, g.scalar, g.tensor, g.sync
     n = len(T.cores)
     others = [T.cores[(rank + d) % n] for d in range(1, n)]
-    prev = T.cores[(rank - 1) % n]
     used = [0]
     evs = []
 
@@ -89,220 +93,282 @@ def rank_program(g, core, T, topo):
             q.wait_ge(e[0], e[1])
             e[2] = 1
 
-    def send(ap_src, ap_dst, dsts, rsem, lsem):
-        m = topo.mask(core, dsts[0])
-        for d in dsts:
+    def send(ap, rsem, lsem):
+        m = topo.mask(core, others[0])
+        for d in others:
             m &= topo.mask(core, d)
         ids = []
-        for d in dsts:
+        for d in others:
             a = topo.addr(d)
             ids.append(DstId(rid=a[0], pnc=a[1]))
-        g.remote_dma_fused([RemoteDMATransfer(dst_ids=ids, dma_engine_mask=m, remote_sem=rsem, srcs=[ap_src],
-                                              dsts=[ap_dst for d in dsts])], local_sem=lsem)
+        g.remote_dma_fused([RemoteDMATransfer(dst_ids=ids, dma_engine_mask=m, remote_sem=rsem, srcs=[ap],
+                                              dsts=[ap for d in others])], local_sem=lsem)
         return bin(m).count("1")
 
     w0, w1 = 512 * rank, 512 * rank + 512
-    at = [0, 32 * NB[0], 512]
+    h0, h1, hn = 36 * rank, 36 * rank + 33, 36 * ((rank + 1) % n)
 
-    def kid(q, h, g2):
-        q.dma_start(T["KR%d" % h][:, g2, :, :], T.kid[g2:8:2, 16 * at[h]:16 * at[h + 1]]).then_inc(T.sem["lK%d" % h], 16)
+    def kid(q, j):
+        h, g2 = j // 2, j % 2
+        q.dma_start(T.KR[:, j, :, :], T.kid[g2:8:2, 512 * R * h:512 * R * (h + 1)]).then_inc(T.sem["lK%d" % j], 16)
 
-    Y.dma_start(T.Lw[:, :], T.lett[:, :]).then_inc(T.sem.lw, 16)
-    kid(S, 0, 1)
-    kid(Y, 0, 0)
+    Y.dma_start(T.RS[:, h0 + 32:h1], T.kid[:, 16:32]).then_inc(T.sem.lR, 16)
+    S.dma_start(T.RS[:, h0:h0 + 32], T.lett[:, :]).then_inc(T.sem.lR, 16)
+    kid(Y, 0)
+    kid(S, 1)
+    kid(Y, 2)
     S.dma_start(T.L4[0:32, :], T.lett[:, :]).then_inc(T.sem.lL, 16)
-    kid(Y, 1, 0)
-    kid(S, 1, 1)
-    S.dma_start(T.T4[0:32, :], T.tid[:, :]).then_inc(T.sem.lT, 16)
-    Y.dma_start(T.T4[32:64, :], T.tid[:, :]).then_inc(T.sem.lT, 16)
-    Y.dma_start(T.T4[64:96, :], T.tid[:, :]).then_inc(T.sem.lT, 16)
+    kid(Y, 3)
+    for j in range(3):
+        S.dma_start(T.T4[32 * j:32 * j + 32, :], T.tid[:, :]).then_inc(T.sem.lT, 16)
 
     imp = {"allow_small_or_imprecise_dtypes": True}
     c0 = event()
     add(c0, g.iota(T.cI[:, 0:1], [[0, 1]], 0, 1))
-    add(c0, g.iota(T.kk[:, 0:6], [[1, 6]], 1, 0, **imp))
-    c1 = one(g.iota(T.tI[:, :], [[1, 144]], -15, 0, **imp))
+    add(c0, g.iota(T.kk[:, :], [[1, 32]], 0, 0, **imp))
     c2 = one(g.iota(T.eR[0:32, :], [[4, 8], [0, 16]], 0, -1, **imp))
     c3 = one(g.iota(T.eE[0:96, :], [[4, 8], [32, 16]], 0, -1, **imp))
-    c4 = one(g.iota(T.eG[:, :], [[16, 8], [0, 16]], 0, -1, **imp))
-    g.wait_ge(T.sem.lw, 16)
-    nH = send(T.Lw[:, :], T.Ln[:, :], [prev], T.sem.aH, T.sem.sH)
-    wait(S, c0)
-    sel = []
-    for c, e, a, o, p in ((c2, T.eR, T.aR, T.RQ, 32), (c3, T.eE, T.aE, T.EQ, 96)):
+    g.wait_ge(T.sem.lR, 32)
+    nH = send(T.RS[:, h0:h1], T.sem.aH, T.sem.sH)
+    c1 = one(g.iota(T.tI[:, :], [[1, 144]], -15, 0, **imp))
+
+    def quarters(c, e, a, o, p):
         wait(S, c)
         ab = event()
         add(ab, S.activation(a[0:p, 0:128], e[0:p, :], ACT.Abs))
         for q in range(1, 4):
-            add(ab, S.activation(a[0:p, 128 * q:128 * q + 128], e[0:p, :], ACT.Abs, bias=T.kk[0:p, q - 1:q]))
+            add(ab, S.activation(a[0:p, 128 * q:128 * q + 128], e[0:p, :], ACT.Abs, bias=T.kk[0:p, q:q + 1]))
         wait(S, ab)
-        sel.append(one(S.activation(o[0:p, :], a[0:p, :], ACT.Relu, scale=-1.0, bias=T.kk[0:p, 0:1])))
+        return one(S.activation(o[0:p, :], a[0:p, :], ACT.Relu, scale=-1.0, bias=T.kk[0:p, 1:2]))
+
+    wait(S, c0)
+    sr = quarters(c2, T.eR, T.aR, T.RQ, 32)
+    se = quarters(c3, T.eE, T.aE, T.EQ, 96)
     wait(V, c0)
     v0 = event()
-    add(v0, V.tensor_scalar(T.cI[:, 1:2], T.cI[:, 0:1], 112, None, A.bitwise_and))
-    add(v0, V.tensor_scalar(T.cI[:, 2:3], T.cI[:, 0:1], 15, None, A.bitwise_and))
-    add(v0, V.tensor_scalar(T.cI[:, 3:4], T.cI[:, 0:1], 12, None, A.bitwise_and))
+    for j, m in ((4, 31), (1, 112), (2, 15), (3, 12)):
+        add(v0, V.tensor_scalar(T.cI[:, j:j + 1], T.cI[:, 0:1], m, None, A.bitwise_and))
     wait(V, v0)
     v1 = one(V.tensor_copy(T.cF[:, :], T.cI[:, :]))
+    pcol, s16, ccol, ocol, ycol = [T.cF[:, j:j + 1] for j in range(5)]
     wait(V, v1)
-    pcol, s16, ccol, ocol = T.cF[:, 0:1], T.cF[:, 1:2], T.cF[:, 2:3], T.cF[:, 3:4]
-    v2 = event()
-    add(v2, V.tensor_scalar(T.cA[:, 0:1], ccol, 2.0, None, A.is_lt))
-    add(v2, V.tensor_scalar(T.cA[:, 1:2], ccol, 2.0, 65536.0, A.is_equal, A.mult))
-    add(v2, V.tensor_scalar(T.cA[:, 2:3], ocol, 128.0, None, A.mult))
-    add(v2, V.tensor_scalar(T.cA[:, 3:4], s16, 0.5, None, A.mult))
-    wait(V, v2, c1)
-    wk = one(V.tensor_scalar(T.wk[:, 0:6], T.kk[:, 0:6], T.cA[:, 1:2], T.cA[:, 0:1], A.mult, A.add))
-    bb = event()
-    add(bb, V.tensor_scalar(T.BO[:, :], T.tI[:, :], s16, T.cA[:, 2:3], A.is_equal, A.mult))
-    add(bb, V.tensor_scalar(T.B[:, :], T.tI[:, :], s16, None, A.is_equal))
-    add(bb, V.tensor_scalar(T.ID[:, :], T.tI[:, 15:143], pcol, None, A.is_equal))
-    wait(V, wk)
-    b2 = event()
-    for k in range(1, 7):
-        add(b2, V.tensor_scalar(T["D%d" % k][:, :], T.tI[:, 8:80], T.cA[:, 3:4], T.wk[:, k - 1:k], A.is_equal, A.mult))
-    wait(V, c4)
-    rg = one(V.tensor_scalar(T.RG[:, :], T.eG[:, :], 0.0, None, A.is_equal))
+    i4 = one(V.tensor_scalar(T.I4[:, :], T.kk[:, :], ycol, None, A.is_equal))
+    ow = one(V.tensor_scalar(T.cA[:, 2:3], ocol, 128.0, None, A.mult))
 
+    cvs = []
+
+    def narrow(j):
+        V.wait_ge(T.sem["lK%d" % j], 16)
+        cvs.append(one(V.tensor_scalar(T.KB[:, j // 2, :, 16 * (j % 2):16 * (j % 2) + 16], T.KR[:, j, :, :], -256.0, None, A.add)))
+
+    def turn(h):
+        wait(P, cvs[2 * h], cvs[2 * h + 1])
+        for b in range(R):
+            for a in range(0, 128, 32):
+                ins = P.matmul(T["ps%d" % (6 + h)][a:a + 32, b:256:R], T.KB[a:a + 32, h, b, :], T.I4[a:a + 32, :], True, True)
+        return one(ins)
+
+    def half(h):
+        wait(V, trs[h])
+        a0 = w0 + 256 * h
+        wcs.append(one(V.tensor_copy(T.W[:, a0:a0 + 256], T["ps%d" % (6 + h)][:, 0:256])))
+        wait(g, wcs[h])
+        return send(T.W[:, a0:a0 + 256], T.sem["aW%d" % h], T.sem["sW%d" % h])
+
+    trs, wcs = [], []
+    narrow(0)
+    narrow(1)
+    wait(P, i4)
+    trs.append(turn(0))
     V.wait_ge(T.sem.lL, 16)
     lr = one(V.tensor_copy(T.L4h[0:32, :], T.L4[0:32, :]))
-    wait(P, lr, sel[0])
+    wait(P, lr, sr)
     for q in range(4):
         ins = P.matmul(T.ps0[:, 128 * q:128 * q + 128], T.RQ[0:32, 128 * q:128 * q + 128], T.L4h[0:32, :], True, True)
     pl = one(ins)
-
-    trs, nW = [], 0
-    for h in range(2):
-        kr, kb, nb = T["KR%d" % h], T["KB%d" % h], NB[h]
-        V.wait_ge(T.sem["lK%d" % h], 32)
-        cv = [one(V.tensor_scalar(kb[:, :, u:u + nb // 2, :], kr[:, :, u:u + nb // 2, :], -256.0, None, A.add)) for u in (0, nb // 2)]
-        tr = event()
-        a0, a1 = w0 + at[h], w0 + at[h + 1]
-        for b in range(nb):
-            if b % (nb // 2) == 0:
-                wait(V, cv[b // (nb // 2)])
-            add(tr, V.transpose(T.W[:, a0 + b:a1:nb], kb[:, :, b, :]))
-        wait(g, tr)
-        nW = send(T.W[:, a0:a1], T.W[:, a0:a1], others, T.sem["aW%d" % h], T.sem["sW%d" % h])
-        trs.append(tr)
+    narrow(2)
+    narrow(3)
+    trs.append(turn(1))
+    nW = half(0)
 
     V.wait_ge(T.sem.lT, 48)
     tf = one(V.tensor_copy(T.T4f[0:96, :], T.T4[0:96, :]))
     wait(S, tf)
     hp = one(S.activation(T.X4[0:64, :], T.T4f[0:64, :], ACT.Copy))
     fp = one(S.activation(T.X4[64:96, :], T.T4f[64:96, :], ACT.Sign))
+    wait(V, c1, ow)
+    bs = event()
+    add(bs, V.tensor_scalar(T.BO[:, :], T.tI[:, :], s16, T.cA[:, 2:3], A.is_equal, A.mult))
+    add(bs, V.tensor_scalar(T.ID[:, :], T.tI[:, 15:143], pcol, None, A.is_equal))
+    half(1)
+    c4 = one(g.iota(T.eG[:, :], [[16, 8], [0, 16]], 0, -1, **imp))
+    c5 = event()
+    add(c5, g.iota(T.tD[:, 0:64], [[1, 64]], -7, 0, **imp))
+    add(c5, g.iota(T.tD[:, 64:136], [[1, 72]], -7, 0, **imp))
     wait(V, pl)
     oh = one(V.tensor_scalar(T.OH[:, 0:512], T.ps0[:, :], ccol, None, A.is_equal))
+    V.wait_ge(T.sem.lR, 32)
+    V.wait_ge(T.sem.aH, nH * len(others))
+    r2 = one(V.tensor_tensor(T.r2[:, :], T.RS[:, 32:72:36], T.RS[:, 104:144:36], A.add))
     wait(V, hp, tf)
     qp = one(V.tensor_tensor(T.X4[32:64, :], T.T4f[32:64, :], T.X4[32:64, :], A.subtract))
-    wait(P, sel[1], hp, fp, qp)
+    wait(P, se, hp, fp, qp)
     for q in range(4):
         ins = P.matmul(T.ps3[:, 128 * q:128 * q + 128], T.EQ[0:96, 128 * q:128 * q + 128], T.X4[0:96, :], True, True)
     pt = one(ins)
-    wait(P, oh, bb)
-    for x in range(16):
-        ins = P.matmul(T.ps2[:, 0:32], T.BO[:, 15 - x:143 - x], T.OH[:, x:512:16], x == 0, x == 15)
-    pb = one(ins)
     wait(S, pt)
     iw = one(S.activation(T.IDW[:, w0:w1], T.ps3[:, :], ACT.Copy))
     wait(g, iw)
-    nI = send(T.IDW[:, w0:w1], T.IDW[:, w0:w1], others, T.sem.aI, T.sem.sI)
-    V.wait_ge(T.sem.aH, nH)
-    ln = one(V.tensor_copy(T.Lnh[:, :], T.Ln[:, 0:8]))
+    nI = send(T.IDW[:, w0:w1], T.sem.aI, T.sem.sI)
+
+    wait(V, r2)
+    rv = one(V.tensor_scalar(T.rv[:, :], T.r2[:, 0:1], T.r2[:, 1:2], T.cA[:, 2:3], A.add, A.add))
+    ln = one(V.tensor_copy(T.Lnh[:, :], T.RS[:, hn:hn + 8]))
+    wait(V, rv)
+    b1 = one(V.tensor_scalar(T.B1[:, :], T.tI[:, :], s16, T.rv[:, 0:1], A.is_equal, A.mult))
+    wait(V, c4)
+    rg = one(V.tensor_scalar(T.RG[:, :], T.eG[:, :], 0.0, None, A.is_equal))
+    v2 = event()
+    add(v2, V.tensor_scalar(T.cA[:, 1:2], ccol, 2.0, 65536.0, A.is_equal, A.mult))
+    add(v2, V.tensor_scalar(T.cA[:, 0:1], ccol, 2.0, None, A.is_lt))
+    add(bs, V.tensor_scalar(T.B[:, :], T.tI[:, :], s16, None, A.is_equal))
+    wait(P, oh, b1)
+    for x in range(16):
+        ins = P.matmul(T.ps1[:, 0:32], T.B1[:, 15 - x:143 - x], T.OH[:, x:512:16], x == 0, x == 15)
+    p1 = one(ins)
     wait(P, ln, rg)
     ph = one(P.matmul(T.ps4[:, 0:8], T.RG[:, :], T.Lnh[:, :], True, True))
-    wait(V, pb)
-    bw1 = one(V.tensor_scalar(T.bw1[:, :], T.ps2[:, 0:32], 1024.0, None, A.add))
-    bw = one(V.tensor_scalar(T.bw[:, :], T.ps2[:, 0:32], 256.0, None, A.add))
+    wait(P, bs)
+    for x in range(16):
+        ins = P.matmul(T.ps2[:, 0:32], T.BO[:, 15 - x:143 - x], T.OH[:, x:512:16], x == 0, x == 15)
+    pb = one(ins)
+    wait(V, p1)
+    l1 = one(V.tensor_copy(T.LS[:, 0:32], T.ps1[:, 0:32]))
     wait(V, ph)
     ohn = one(V.tensor_scalar(T.OH[:, 512:520], T.ps4[:, 0:8], ccol, None, A.is_equal))
 
-    V.wait_ge(T.sem.aW0, nW * len(others))
-    wait(V, trs[0])
-    rv = one(V.tensor_reduce(T.rv[:, :], T.W[:, 1:2048:512], AxisListType.X, A.add))
-    wait(V, rv)
-    b1 = one(V.tensor_scalar(T.B1[:, :], T.tI[:, :], s16, T.rv[:, 0:1], A.is_equal, A.mult))
+    wait(S, c5, v1)
+    ba = one(S.activation(T.cA[:, 6:7], T.kk[:, 1:2], ACT.Copy, scale=256.0))
+    s0 = one(S.activation(T.cA[:, 3:4], s16, ACT.Copy, scale=0.5))
+    wait(S, v2)
+    s1 = event()
+    add(s1, S.activation(T.wk[:, 0:6], T.kk[:, 1:7], ACT.Identity, scale=T.cA[:, 1:2], bias=T.cA[:, 0:1]))
+    wait(S, s0)
+    s2 = one(S.activation(T.pA[:, :], T.tD[:, :], ACT.Abs, scale=-1.0, bias=T.cA[:, 3:4]))
+    add(s1, S.activation(T.cA[:, 4:5], T.cA[:, 1:2], ACT.Copy, scale=6.0 / 65536.0))
+    wait(S, s2)
+    s3 = one(S.activation(T.pP[:, :], T.pA[:, :], ACT.Relu, scale=-1.0, bias=T.kk[:, 1:2]))
+    add(s1, S.activation(T.cA[:, 5:6], T.cA[:, 1:2], ACT.Copy, scale=6.0))
+    wait(S, pb, ba)
+    bw = one(S.activation(T.bw[:, :], T.ps2[:, 0:32], ACT.Identity, bias=T.cA[:, 6:7]))
+    wait(S, s1, s3)
+    sel = event()
+    for k in range(1, 6):
+        add(sel, S.activation(T["D%d" % k][:, :], T.pP[:, :], ACT.Copy, scale=T.wk[:, k - 1:k]))
+    add(sel, S.activation(T.D6[:, 0:64], T.pP[:, 0:64], ACT.Copy, scale=T.cA[:, 5:6]))
+    add(sel, S.activation(T.D6[:, 64:136], T.pP[:, 64:136], ACT.Copy, scale=T.cA[:, 4:5]))
+    add(sel, S.activation(T.DI[:, :], T.pP[:, 64:136], ACT.Copy, scale=T.cA[:, 0:1]))
+
     S.wait_ge(T.sem.aI, nI * len(others))
     wait(S, iw)
-    bank = {1: T.ps4, 2: T.ps5, 3: T.ps6, 4: T.ps7, 5: T.ps3, 6: T.ps0}
+    bank = {1: T.ps4, 2: T.ps5, 3: T.ps6, 4: T.ps7, 5: T.ps3}
     acc = [T.ps1, T.ps2]
-    gat, gid, idp, ky, ls = {}, {}, {}, {}, {}
+    gat, gid, idp, ky, ls = {}, {}, {}, {}, {(1, 0): l1, (1, 1): l1}
 
-    def idstep(k, bs, es):
-        wait(P, *es)
+    def idsum(out, m, D, k, bs):
         for b in bs:
-            ins = P.matmul(bank[k][0:64, 0:64], T["D%d" % k][:, 7 - b:71 - b], T["G%d" % k][:, 64 * b:64 * b + 64], b == 0, b == 7)
-        if b == 7:
-            idp[k] = one(ins)
+            ins = P.matmul(out[0:m, 0:64], D[:, 7 - b:7 - b + m], T["G%d" % k][:, 64 * b:64 * b + 64], b == 0, b == 7)
+        return ins
+
+    def idstep(m):
+        wait(P, gid[m], sel)
+        if m == 1:
+            wait(P, ohn)
+        idp[m] = one(idsum(bank[m], 128, T["D%d" % m], m, range(8)))
 
     def keystep(k):
         wait(V, idp[k])
+        o = T.keyI if k == 5 else T.key
         if k == 1:
-            ky[k] = one(V.tensor_copy(T.key[0:64, :], bank[k][0:64, 0:64]))
+            ky[k] = one(V.tensor_copy(o[:, :], bank[k][:, 0:64]))
         else:
             wait(V, ky[k - 1])
-            ky[k] = one(V.tensor_tensor(T.key[0:64, :], T.key[0:64, :], bank[k][0:64, 0:64], A.max))
+            ky[k] = one(V.tensor_tensor(o[:, :], T.key[:, :], bank[k][:, 0:64], A.max))
 
-    wait(P, bw1, bw, ohn)
-    ids = {4: [1], 5: [2, 3], 6: [4, 5]}
-    keys = {(5, 0): [1], (6, 0): [2], (6, 1): [3]}
-    for k in range(1, 7):
+    def gather(k, s):
+        c = 32 * k - 64 + 16 * s
+        wait(V, ls[k - 1, s])
+        gat[k, s] = one(V.tensor_tensor(T["RM%d" % s][:, :], T.W[:, :].indirect(T.LS[:, c:c + 16]),
+                                        T.OH[:, 256 * s + k - 1:256 * s + k + 255], A.mult))
+
+    def idgather(k):
+        wait(S, ls[k, 0], ls[k, 1])
+        gid[k] = one(S.activation(T["G%d" % k][:, :], T.IDW[:, :].indirect(T.LS[:, 32 * k - 32:32 * k]), ACT.Copy))
+
+    idgather(1)
+    for h in range(2):
+        V.wait_ge(T.sem["aW%d" % h], nW * len(others))
+    wait(V, wcs[0], wcs[1], oh)
+    gather(2, 0)
+    wait(V, ohn)
+    gather(2, 1)
+    wait(P, bw)
+    begin = {4: 1, 5: 2, 6: 3}
+    keys = {(4, 1): 1, (5, 1): 2, (6, 0): 3, (6, 1): 4}
+    for k in range(2, 7):
+        if k in begin:
+            idstep(begin[k])
         pm = []
         for s in range(2):
-            if k > 1:
-                wait(P, ls[k - 1, s])
-            P.matmul(acc[s][:, 0:16], T.ID[:, :], (T.bw1 if k == 1 else T.bw)[:, 16 * s:16 * s + 16], True, False)
-            wait(P, b1 if k == 1 else gat[k, s])
+            wait(P, ls[k - 1, s])
+            P.matmul(acc[s][:, 0:16], T.ID[:, :], T.bw[:, 16 * s:16 * s + 16], True, False)
+            wait(P, gat[k, s])
             for x in range(16):
-                if k == 1:
-                    ins = P.matmul(acc[s][:, 0:16], T.B1[:, 15 - x:143 - x], T.OH[:, 256 * s + x:256 * s + 256:16], False, x == 15)
-                else:
-                    ins = P.matmul(acc[s][:, 0:16], T.B[:, 15 - x:143 - x], T["RM%d" % s][:, x:256:16], False, x == 15)
+                ins = P.matmul(acc[s][:, 0:16], T.B[:, 15 - x:143 - x], T["RM%d" % s][:, x:256:16], False, x == 15)
             pm.append(one(ins))
-        if k == 4:
-            wait(P, b2)
-        for m in ids.get(k, []):
-            idstep(m, range(8), [gid[m]])
+        if k == 6:
+            idstep(4)
+            idstep(5)
         for s in range(2):
             c = 32 * k - 32 + 16 * s
             wait(V, pm[s])
             ls[k, s] = one(V.tensor_copy(T.LS[:, c:c + 16], acc[s][:, 0:16]))
-            for m in keys.get((k, s), []):
-                keystep(m)
-            if k == 1 and s == 0:
-                wait(V, ohn, trs[1])
-                V.wait_ge(T.sem.aW1, nW * len(others))
-            wait(V, ls[k, s])
+            if (k, s) in keys:
+                keystep(keys[k, s])
             if k < 6:
-                gat[k + 1, s] = one(V.tensor_tensor(T["RM%d" % s][:, :], T.W[:, :].indirect(T.LS[:, c:c + 16]),
-                                                    T.OH[:, 256 * s + k:256 * s + k + 256], A.mult))
+                gather(k + 1, s)
             elif s == 0:
                 V.wait_ge(T.sem.aI, nI * len(others))
-                wait(V, iw)
+                wait(V, iw, ls[6, 0])
                 i0 = one(V.tensor_copy(T.G6[:, 0:256], T.IDW[:, :].indirect(T.LS[:, c:c + 16])))
-                idstep(6, range(4), [i0])
             else:
-                wait(S, ls[k, 1])
-                i1 = one(V.tensor_copy(T.G6[:, 256:384], T.IDW[:, :].indirect(T.LS[:, c:c + 8])))
-                i2 = one(S.activation(T.G6[:, 384:512], T.IDW[:, :].indirect(T.LS[:, c + 8:c + 16]), ACT.Copy))
-                idstep(6, range(4, 8), [i1, i2])
+                wait(S, ls[6, 1])
+                wait(V, ls[6, 1])
+                i1 = one(V.tensor_copy(T.G6[:, 256:352], T.IDW[:, :].indirect(T.LS[:, c:c + 6])))
+                i2 = one(S.activation(T.G6[:, 352:512], T.IDW[:, :].indirect(T.LS[:, c + 6:c + 16]), ACT.Copy))
         if k < 6:
-            wait(S, ls[k, 0], ls[k, 1])
-            gid[k] = one(S.activation(T["G%d" % k][:, :], T.IDW[:, :].indirect(T.LS[:, 32 * k - 32:32 * k]), ACT.Copy))
-    keystep(4)
+            idgather(k)
+    zb, ib = T.ps0, T.ps1
+    wait(P, i0)
+    idsum(zb, 128, T.D6, 6, range(4))
+    idsum(ib, 64, T.DI, 6, range(4))
+    wait(P, i1, i2)
+    pz = one(idsum(zb, 128, T.D6, 6, range(4, 8)))
+    pi = one(idsum(ib, 64, T.DI, 6, range(4, 8)))
     keystep(5)
-    wait(V, idp[6], ky[5])
-    kf = one(V.tensor_tensor(T.keyI[0:64, :], T.key[0:64, :], bank[6][0:64, 0:64], A.max))
-    wait(V, kf)
-    od = event()
-    add(od, V.tensor_scalar(T.OI[0:64, 0:64], T.keyI[0:64, :], 16, None, A.arith_shift_right))
-    add(od, V.tensor_scalar(T.OI[0:64, 64:128], T.keyI[0:64, :], 65535, None, A.bitwise_and))
-    wait(V, od)
-    of = one(V.tensor_copy(T.OF[0:64, :], T.OI[0:64, :]))
-    wait(Y, of)
-    Y.dma_start(T.ylen[:, :], T.OF[0:64, 0:64]).then_inc(T.sem.oY, 16)
-    wait(S, of)
-    S.dma_start(T.yid[:, :], T.OF[0:64, 64:128]).then_inc(T.sem.oY, 16)
+    wait(V, ky[5])
+    k5 = event()
+    add(k5, V.tensor_scalar(T.idI[0:64, :], T.keyI[0:64, :], 65535, None, A.bitwise_and))
+    add(k5, V.tensor_scalar(T.kI[64:128, :], T.keyI[64:128, :], 16, None, A.arith_shift_right))
+    wait(V, pz, k5)
+    ue = one(V.tensor_tensor(T.u[0:64, :], T.idI[0:64, :], zb[0:64, 0:64], A.subtract))
+    ol = one(V.tensor_tensor(T.OL[64:128, :], T.kI[64:128, :], zb[64:128, 0:64], A.max))
+    wait(V, pi, ue)
+    od = one(V.tensor_tensor(T.OD[0:64, :], T.u[0:64, :], ib[0:64, 0:64], A.max))
+    wait(S, ol)
+    S.dma_start(T.ylen[:, :], T.OL[64:128, :]).then_inc(T.sem.oY, 16)
+    wait(Y, od)
+    Y.dma_start(T.yid[:, :], T.OD[0:64, :]).then_inc(T.sem.oY, 16)
     g.wait_ge(T.sem.sH, nH)
     g.wait_ge(T.sem.sW0, nW)
     g.wait_ge(T.sem.sW1, nW)

@@ -1,49 +1,55 @@
 from concourse.bass import DstId, RemoteDMATransfer
-from concourse.mybir import AluOpType, AxisListType, ActivationFunctionType
+from concourse.mybir import AluOpType, ActivationFunctionType
 
 R = 8
 
 SCRATCH = {
     "KR": ("sbuf", [128, 4, R, 16], "int32"),
-    "KB": ("sbuf", [128, 2, R, 32], "bfloat16"),
-    "I4": ("sbuf", [128, 32], "bfloat16"),
+    "KB": ("sbuf", [128, R, 64], "bfloat16"),
+    "I64": ("sbuf", [128, 64], "bfloat16"),
     "W": ("sbuf", [128, 2048], "bfloat16"),
     "IDW": ("sbuf", [128, 2048], "bfloat16"),
-    "RS": ("sbuf", [128, 144], "int32"),
-    "r2": ("sbuf", [128, 2], "float32"),
-    "rv": ("sbuf", [128, 1], "float32"),
-    "Lnh": ("sbuf", [128, 8], "float16"),
+    "T3": ("sbuf", [128, 256], "float32"),
+    "KT": ("sbuf", [128, 256], "bfloat16"),
+    "R1": ("sbuf", [128, 2], "uint16"),
+    "D2": ("sbuf", [128, 16], "uint16"),
+    "I1": ("sbuf", [128, 16], "float32"),
+    "I2": ("sbuf", [128, 64], "bfloat16"),
     "L4": ("sbuf", [128, 128], "int32"),
+    "LN": ("sbuf", [128, 8], "int32"),
     "L4h": ("sbuf", [128, 128], "bfloat16"),
+    "Lnh": ("sbuf", [128, 8], "bfloat16"),
     "T4": ("sbuf", [128, 128], "int32"),
     "T4f": ("sbuf", [128, 128], "float32"),
     "X4": ("sbuf", [128, 128], "bfloat16"),
-    "OH": ("sbuf", [128, 520], "float16"),
+    "OH": ("sbuf", [128, 528], "bfloat16"),
     "RM0": ("sbuf", [128, 256], "float16"),
     "RM1": ("sbuf", [128, 256], "float16"),
-    "LS": ("sbuf", [128, 192], "uint16"),
-    "cI": ("sbuf", [128, 5], "int32"),
-    "cF": ("sbuf", [128, 5], "float32"),
-    "cA": ("sbuf", [128, 8], "float32"),
+    "LS": ("sbuf", [128, 160], "uint16"),
+    "LI": ("sbuf", [128, 32], "int32"),
+    "LO": ("sbuf", [128, 32], "int32"),
+    "cI": ("sbuf", [128, 6], "int32"),
+    "cF": ("sbuf", [128, 6], "float32"),
+    "cA": ("sbuf", [128, 32], "float32"),
     "tI": ("sbuf", [128, 144], "bfloat16"),
-    "tD": ("sbuf", [128, 136], "float32"),
+    "pL": ("sbuf", [128, 144], "float32"),
+    "pM": ("sbuf", [128, 144], "float32"),
     "pA": ("sbuf", [128, 136], "float32"),
     "pP": ("sbuf", [128, 136], "float32"),
-    "eR": ("sbuf", [128, 128], "float32"),
-    "eE": ("sbuf", [128, 128], "float32"),
-    "eG": ("sbuf", [128, 128], "bfloat16"),
-    "aR": ("sbuf", [128, 512], "float32"),
-    "aE": ("sbuf", [128, 512], "float32"),
+    "eR": ("sbuf", [128, 128], "bfloat16"),
+    "eE": ("sbuf", [128, 128], "bfloat16"),
     "RQ": ("sbuf", [128, 512], "bfloat16"),
     "EQ": ("sbuf", [128, 512], "bfloat16"),
-    "kk": ("sbuf", [128, 32], "float32"),
-    "wk": ("sbuf", [128, 8], "float32"),
-    "RG": ("sbuf", [128, 128], "float16"),
+    "kk": ("sbuf", [128, 10], "float32"),
     "B": ("sbuf", [128, 144], "float16"),
-    "B1": ("sbuf", [128, 144], "float16"),
-    "BO": ("sbuf", [128, 144], "float16"),
+    "BL": ("sbuf", [128, 144], "bfloat16"),
+    "BC": ("sbuf", [128, 144], "bfloat16"),
+    "BD": ("sbuf", [128, 144], "bfloat16"),
     "ID": ("sbuf", [128, 128], "bfloat16"),
     "bw": ("sbuf", [128, 32], "bfloat16"),
+    "D": ("sbuf", [128, 136], "bfloat16"),
+    "D1": ("sbuf", [128, 136], "bfloat16"),
+    "D6": ("sbuf", [128, 136], "bfloat16"),
     "DI": ("sbuf", [128, 72], "bfloat16"),
     "key": ("sbuf", [128, 64], "float32"),
     "keyI": ("sbuf", [128, 64], "int32"),
@@ -53,13 +59,12 @@ SCRATCH = {
     "OL": ("sbuf", [128, 64], "float32"),
     "OD": ("sbuf", [128, 64], "float32"),
 }
-for _k in range(1, 7):
-    SCRATCH["D%d" % _k] = ("sbuf", [128, 136], "bfloat16")
+for _k in range(2, 7):
     SCRATCH["G%d" % _k] = ("sbuf", [128, 512], "bfloat16")
 for _k in range(8):
     SCRATCH["ps%d" % _k] = ("psum", [128, 512], "float32")
 
-SEMAPHORES = ["lL", "lR", "lT", "lK0", "lK1", "lK2", "lK3", "aH", "aW0", "aW1", "aI", "sH", "sW0", "sW1", "sI", "oY"] + ["e%d" % k for k in range(134)]
+SEMAPHORES = ["lL", "lT", "lK0", "lK1", "lK2", "lK3", "aH", "aT", "aW", "aI", "aK", "sH", "sT", "sW", "sI", "sK", "oY"] + ["e%d" % k for k in range(130)]
 
 
 def rank_program(g, core, T, topo):
@@ -93,198 +98,226 @@ def rank_program(g, core, T, topo):
             q.wait_ge(e[0], e[1])
             e[2] = 1
 
-    def send(ap, rsem, lsem):
-        m = topo.mask(core, others[0])
-        for d in others:
+    def send(dst, src, rsem, lsem, cores):
+        m = topo.mask(core, cores[0])
+        for d in cores:
             m &= topo.mask(core, d)
         ids = []
-        for d in others:
+        for d in cores:
             a = topo.addr(d)
             ids.append(DstId(rid=a[0], pnc=a[1]))
-        g.remote_dma_fused([RemoteDMATransfer(dst_ids=ids, dma_engine_mask=m, remote_sem=rsem, srcs=[ap],
-                                              dsts=[ap for d in others])], local_sem=lsem)
+        g.remote_dma_fused([RemoteDMATransfer(dst_ids=ids, dma_engine_mask=m, remote_sem=rsem, srcs=[src],
+                                              dsts=[dst for d in cores])], local_sem=lsem)
         return bin(m).count("1")
 
     w0, w1 = 512 * rank, 512 * rank + 512
-    h0, h1, hn = 36 * rank, 36 * rank + 33, 36 * ((rank + 1) % n)
+    t0, t1 = 64 * rank, 64 * rank + 64
 
     def kid(q, j):
-        h, g2 = j // 2, j % 2
-        q.dma_start(T.KR[:, j, :, :], T.kid[g2:8:2, 512 * R * h:512 * R * (h + 1)]).then_inc(T.sem["lK%d" % j], 16)
+        q.dma_start(T.KR[:, j, :, :], T.kid[j:8:4, :]).then_inc(T.sem["lK%d" % j], 16)
 
-    Y.dma_start(T.RS[:, h0 + 32:h1], T.kid[:, 16:32]).then_inc(T.sem.lR, 16)
-    S.dma_start(T.RS[:, h0:h0 + 32], T.lett[:, :]).then_inc(T.sem.lR, 16)
     kid(Y, 0)
     kid(S, 1)
-    kid(Y, 2)
     S.dma_start(T.L4[0:32, :], T.lett[:, :]).then_inc(T.sem.lL, 16)
+    kid(Y, 2)
     kid(Y, 3)
     for j in range(3):
-        S.dma_start(T.T4[32 * j:32 * j + 32, :], T.tid[:, :]).then_inc(T.sem.lT, 16)
+        Y.dma_start(T.T4[32 * j:32 * j + 32, :], T.tid[:, :]).then_inc(T.sem.lT, 16)
 
     imp = {"allow_small_or_imprecise_dtypes": True}
-    c0 = event()
-    add(c0, g.iota(T.cI[:, 0:1], [[0, 1]], 0, 1))
-    add(c0, g.iota(T.kk[:, :], [[1, 32]], 0, 0, **imp))
-    c2 = one(g.iota(T.eR[0:32, :], [[4, 8], [0, 16]], 0, -1, **imp))
-    c3 = one(g.iota(T.eE[0:96, :], [[4, 8], [32, 16]], 0, -1, **imp))
-    g.wait_ge(T.sem.lR, 32)
-    nH = send(T.RS[:, h0:h1], T.sem.aH, T.sem.sH)
+    c0 = one(g.iota(T.cI[:, 0:2], [[8, 2]], 0, 1))
     c1 = one(g.iota(T.tI[:, :], [[1, 144]], -15, 0, **imp))
-
-    def quarters(c, e, a, o, p):
-        wait(S, c)
-        ab = event()
-        add(ab, S.activation(a[0:p, 0:128], e[0:p, :], ACT.Abs))
-        for q in range(1, 4):
-            add(ab, S.activation(a[0:p, 128 * q:128 * q + 128], e[0:p, :], ACT.Abs, bias=T.kk[0:p, q:q + 1]))
-        wait(S, ab)
-        return one(S.activation(o[0:p, :], a[0:p, :], ACT.Relu, scale=-1.0, bias=T.kk[0:p, 1:2]))
-
-    wait(S, c0)
-    sr = quarters(c2, T.eR, T.aR, T.RQ, 32)
-    se = quarters(c3, T.eE, T.aE, T.EQ, 96)
-    wait(V, c0)
+    ck = one(g.iota(T.kk[:, :], [[1, 10]], 0, 0, **imp))
+    c2 = one(g.iota(T.eR[0:32, :], [[4, 8], [0, 16]], 0, -1, **imp))
     v0 = event()
-    for j, m in ((4, 31), (1, 112), (2, 15), (3, 12)):
-        add(v0, V.tensor_scalar(T.cI[:, j:j + 1], T.cI[:, 0:1], m, None, A.bitwise_and))
-    wait(V, v0)
-    v1 = one(V.tensor_copy(T.cF[:, :], T.cI[:, :]))
-    pcol, s16, ccol, ocol, ycol = [T.cF[:, j:j + 1] for j in range(5)]
+    add(v0, V.memset(T.L4[32:64, 0:8], 0))
+    add(v0, V.memset(T.L4[64:128, 0:8], 0))
+    wait(g, v0)
+    g.wait_ge(T.sem.lL, 16)
+    nH = send(T.LN[:, 0:8], T.L4[:, 0:8], T.sem.aH, T.sem.sH, [T.cores[(rank + n - 1) % n]])
+    c3 = one(g.iota(T.eE[0:96, :], [[4, 8], [0, 2], [32, 8]], 0, -1, **imp))
+
+    wait(V, c0)
+    v1 = event()
+    add(v1, V.tensor_scalar(T.cI[:, 4:5], T.cI[:, 0:1], 63, None, A.bitwise_and))
+    add(v1, V.tensor_scalar(T.cI[:, 2:4], T.cI[:, 0:2], 15, None, A.bitwise_and))
+    add(v1, V.tensor_scalar(T.cI[:, 5:6], T.cI[:, 0:1], 112, None, A.bitwise_and))
     wait(V, v1)
-    i4 = one(V.tensor_scalar(T.I4[:, :], T.kk[:, :], ycol, None, A.is_equal))
-    ow = one(V.tensor_scalar(T.cA[:, 2:3], ocol, 128.0, None, A.mult))
+    cf = one(V.tensor_copy(T.cF[:, :], T.cI[:, :]))
+    pcol, ccol, ycol, s16 = [T.cF[:, j:j + 1] for j in (0, 2, 4, 5)]
+    cc = T.cF[:, 2:4]
+    wait(V, cf, c1)
+    i64 = one(V.tensor_scalar(T.I64[:, :], T.tI[:, 15:79], ycol, None, A.is_equal))
+
+    wait(S, ck, cf)
+    q0 = event()
+    add(q0, S.activation(T.cA[:, 0:1], ccol, ACT.Copy, scale=17.0))
+    add(q0, S.activation(T.cA[:, 1:2], ccol, ACT.Copy, scale=-1.0))
+    add(q0, S.activation(T.cA[:, 3:4], s16, ACT.Identity, scale=-17.0, bias=T.kk[:, 1:2]))
+    add(q0, S.activation(T.cA[:, 2:3], ccol, ACT.Copy, scale=16.0))
+    wait(S, q0, c1)
+    ql = one(S.activation(T.pL[:, :], T.tI[:, :], ACT.Abs, scale=17.0, bias=T.cA[:, 3:4]))
+    wait(S, ql)
+    bl = one(S.activation(T.BL[:, :], T.pL[:, :], ACT.Relu, scale=T.cA[:, 1:2], bias=T.cA[:, 0:1]))
 
     cvs = []
-
-    def narrow(j):
+    for j in range(4):
         V.wait_ge(T.sem["lK%d" % j], 16)
-        cvs.append(one(V.tensor_scalar(T.KB[:, j // 2, :, 16 * (j % 2):16 * (j % 2) + 16], T.KR[:, j, :, :], -256.0, None, A.add)))
-
-    def turn(h):
-        wait(P, cvs[2 * h], cvs[2 * h + 1])
-        for b in range(R):
-            for a in range(0, 128, 32):
-                ins = P.matmul(T["ps%d" % (6 + h)][a:a + 32, b:256:R], T.KB[a:a + 32, h, b, :], T.I4[a:a + 32, :], True, True)
-        return one(ins)
-
-    def half(h):
-        wait(V, trs[h])
-        a0 = w0 + 256 * h
-        wcs.append(one(V.tensor_copy(T.W[:, a0:a0 + 256], T["ps%d" % (6 + h)][:, 0:256])))
-        wait(g, wcs[h])
-        return send(T.W[:, a0:a0 + 256], T.sem["aW%d" % h], T.sem["sW%d" % h])
-
-    trs, wcs = [], []
-    narrow(0)
-    narrow(1)
-    wait(P, i4)
-    trs.append(turn(0))
+        cvs.append(one(V.tensor_scalar(T.KB[:, :, 16 * j:16 * j + 16], T.KR[:, j, :, :], -256.0, None, A.add)))
+    wait(P, i64, *cvs)
+    tr = []
+    for h, out in ((0, T.ps5), (1, T.ps7)):
+        for b in range(h, R, 2):
+            for a in (0, 64):
+                ins = P.matmul(out[a:a + 64, b // 2:256:R // 2], T.KB[a:a + 64, b, :], T.I64[a:a + 64, :], True, True)
+        tr.append(one(ins))
+    wait(S, tr[0])
+    we = one(S.activation(T.W[:, w0:w1:2], T.ps5[:, 0:256], ACT.Copy))
     V.wait_ge(T.sem.lL, 16)
     lr = one(V.tensor_copy(T.L4h[0:32, :], T.L4[0:32, :]))
+    wait(V, c2)
+    sr = event()
+    for q in range(4):
+        add(sr, V.tensor_scalar(T.RQ[0:32, 128 * q:128 * q + 128], T.eR[0:32, :], float(-q), None, A.is_equal))
+    V.wait_ge(T.sem.lT, 48)
+    tf = one(V.tensor_copy(T.T4f[0:96, :], T.T4[0:96, :]))
     wait(P, lr, sr)
     for q in range(4):
         ins = P.matmul(T.ps0[:, 128 * q:128 * q + 128], T.RQ[0:32, 128 * q:128 * q + 128], T.L4h[0:32, :], True, True)
     pl = one(ins)
-    narrow(2)
-    narrow(3)
-    trs.append(turn(1))
-    nW = half(0)
+    wait(V, tr[1])
+    r1 = one(V.tensor_scalar(T.R1[:, 0:1], T.ps7[:, 0:1], 256.0, None, A.add))
+    wc = one(V.tensor_copy(T.W[:, w0 + 1:w1:2], T.ps7[:, 0:256]))
+    wait(V, r1, we, wc)
+    d2 = one(V.tensor_scalar(T.D2[:, :], T.W[:, w0:w1].indirect(T.R1[:, 0:1]), 256.0, None, A.add))
+    wait(V, d2)
+    t3 = one(V.tensor_scalar(T.T3[:, t0:t1], T.W[:, w0:w1].indirect(T.D2[:, 4 * rank:4 * rank + 4]), 256.0 + w0, None, A.add))
+    wait(g, t3)
+    nT = send(T.T3[:, t0:t1], T.T3[:, t0:t1], T.sem.aT, T.sem.sT, others)
+    wait(g, we, wc)
+    nW = send(T.W[:, w0:w1], T.W[:, w0:w1], T.sem.aW, T.sem.sW, others)
 
-    V.wait_ge(T.sem.lT, 48)
-    tf = one(V.tensor_copy(T.T4f[0:96, :], T.T4[0:96, :]))
     wait(S, tf)
     hp = one(S.activation(T.X4[0:64, :], T.T4f[0:64, :], ACT.Copy))
     fp = one(S.activation(T.X4[64:96, :], T.T4f[64:96, :], ACT.Sign))
-    wait(V, c1, ow)
-    bs = event()
-    add(bs, V.tensor_scalar(T.BO[:, :], T.tI[:, :], s16, T.cA[:, 2:3], A.is_equal, A.mult))
-    add(bs, V.tensor_scalar(T.ID[:, :], T.tI[:, 15:143], pcol, None, A.is_equal))
-    half(1)
-    c4 = one(g.iota(T.eG[:, :], [[16, 8], [0, 16]], 0, -1, **imp))
-    c5 = event()
-    add(c5, g.iota(T.tD[:, 0:64], [[1, 64]], -7, 0, **imp))
-    add(c5, g.iota(T.tD[:, 64:136], [[1, 72]], -7, 0, **imp))
+    q1 = event()
+    add(q1, S.activation(T.cA[:, 5:6], s16, ACT.Copy, scale=-1.0))
+    add(q1, S.activation(T.cA[:, 14:15], ccol, ACT.Copy, scale=-16.0))
+    add(q1, S.activation(T.cA[:, 4:5], s16, ACT.Identity, scale=-0.5, bias=T.kk[:, 8:9]))
+    wait(S, q1)
+    q2 = one(S.activation(T.pM[:, :], T.tI[:, :], ACT.Abs, bias=T.cA[:, 5:6]))
+    wait(S, q2)
+    bc = event()
+    add(bc, S.activation(T.BC[:, :], T.pM[:, :], ACT.Relu, scale=T.cA[:, 1:2], bias=ccol))
+    add(bc, S.activation(T.BD[:, :], T.pM[:, :], ACT.Relu, scale=T.cA[:, 14:15], bias=T.cA[:, 2:3]))
+
     wait(V, pl)
-    oh = one(V.tensor_scalar(T.OH[:, 0:512], T.ps0[:, :], ccol, None, A.is_equal))
-    V.wait_ge(T.sem.lR, 32)
-    V.wait_ge(T.sem.aH, nH * len(others))
-    r2 = one(V.tensor_tensor(T.r2[:, :], T.RS[:, 32:72:36], T.RS[:, 104:144:36], A.add))
+    oa = one(V.tensor_scalar(T.OH[:, 0:272], T.ps0[:, 0:272], ccol, None, A.is_equal))
+    wait(V, c3)
+    se = event()
+    for q in range(4):
+        add(se, V.tensor_scalar(T.EQ[0:96, 128 * q:128 * q + 128], T.eE[0:96, :], float(-q), None, A.is_equal))
     wait(V, hp, tf)
     qp = one(V.tensor_tensor(T.X4[32:64, :], T.T4f[32:64, :], T.X4[32:64, :], A.subtract))
-    wait(P, se, hp, fp, qp)
-    for q in range(4):
-        ins = P.matmul(T.ps3[:, 128 * q:128 * q + 128], T.EQ[0:96, 128 * q:128 * q + 128], T.X4[0:96, :], True, True)
-    pt = one(ins)
-    wait(S, pt)
-    iw = one(S.activation(T.IDW[:, w0:w1], T.ps3[:, :], ACT.Copy))
-    wait(g, iw)
-    nI = send(T.IDW[:, w0:w1], T.sem.aI, T.sem.sI)
+    ob = one(V.tensor_scalar(T.OH[:, 272:512], T.ps0[:, 272:512], ccol, None, A.is_equal))
+    V.wait_ge(T.sem.aH, nH)
+    ln = one(V.tensor_copy(T.Lnh[0:32, :], T.LN[0:32, :]))
+    bs = one(V.tensor_scalar(T.B[:, :], T.tI[:, :], s16, None, A.is_equal))
 
-    wait(V, r2)
-    rv = one(V.tensor_scalar(T.rv[:, :], T.r2[:, 0:1], T.r2[:, 1:2], T.cA[:, 2:3], A.add, A.add))
-    ln = one(V.tensor_copy(T.Lnh[:, :], T.RS[:, hn:hn + 8]))
-    wait(V, rv)
-    b1 = one(V.tensor_scalar(T.B1[:, :], T.tI[:, :], s16, T.rv[:, 0:1], A.is_equal, A.mult))
-    wait(V, c4)
-    rg = one(V.tensor_scalar(T.RG[:, :], T.eG[:, :], 0.0, None, A.is_equal))
-    v2 = event()
-    add(v2, V.tensor_scalar(T.cA[:, 1:2], ccol, 2.0, 65536.0, A.is_equal, A.mult))
-    add(v2, V.tensor_scalar(T.cA[:, 0:1], ccol, 2.0, None, A.is_lt))
-    add(bs, V.tensor_scalar(T.B[:, :], T.tI[:, :], s16, None, A.is_equal))
-    wait(P, oh, b1)
-    for x in range(16):
-        ins = P.matmul(T.ps1[:, 0:32], T.B1[:, 15 - x:143 - x], T.OH[:, x:512:16], x == 0, x == 15)
-    p1 = one(ins)
-    wait(P, ln, rg)
-    ph = one(P.matmul(T.ps4[:, 0:8], T.RG[:, :], T.Lnh[:, :], True, True))
-    wait(P, bs)
-    for x in range(16):
-        ins = P.matmul(T.ps2[:, 0:32], T.BO[:, 15 - x:143 - x], T.OH[:, x:512:16], x == 0, x == 15)
-    pb = one(ins)
-    wait(V, p1)
-    l1 = one(V.tensor_copy(T.LS[:, 0:32], T.ps1[:, 0:32]))
+    acc = [T.ps1, T.ps2]
+    pts = []
+
+    def ids():
+        wait(P, se, hp, fp, qp)
+        for q in range(4):
+            ins = P.matmul(T.ps3[:, 128 * q:128 * q + 128], T.EQ[0:96, 128 * q:128 * q + 128], T.X4[0:96, :], True, True)
+        pts.append(one(ins))
+
+    def pairs(s):
+        a = 256 * s
+        for x in range(1, 16):
+            P.matmul(acc[s][:, 0:16], T.BL[:, 15 - x:143 - x], T.OH[:, a + x:a + 256:16], x == 1, False)
+        if s == 0:
+            ids()
+        wait(P, bc)
+        P.matmul(acc[s][:, 0:16], T.BD[:, 15:143], T.OH[:, a:a + 256:16], False, False)
+        return one(P.matmul(acc[s][:, 0:16], T.BC[:, 0:128], T.OH[:, a + 16:a + 257:16], False, True))
+
+    wait(P, oa, bl)
+    pairs0 = pairs(0)
+    wait(P, ln)
+    ph = one(P.matmul(T.ps4[:, 0:8], T.RQ[0:32, 0:128], T.Lnh[0:32, :], True, True))
+
+    ls = {}
+
+    def copylist(k, s):
+        c = 32 * k - 64 + 16 * s
+        ls[k, s] = one(V.tensor_copy(T.LS[:, c:c + 16], acc[s][:, 0:16]))
+
+    wait(V, pairs0)
+    copylist(2, 0)
     wait(V, ph)
     ohn = one(V.tensor_scalar(T.OH[:, 512:520], T.ps4[:, 0:8], ccol, None, A.is_equal))
+    wait(P, ob, ohn)
+    pairs1 = pairs(1)
 
-    wait(S, c5, v1)
-    ba = one(S.activation(T.cA[:, 6:7], T.kk[:, 1:2], ACT.Copy, scale=256.0))
-    s0 = one(S.activation(T.cA[:, 3:4], s16, ACT.Copy, scale=0.5))
-    wait(S, v2)
-    s1 = event()
-    add(s1, S.activation(T.wk[:, 0:6], T.kk[:, 1:7], ACT.Identity, scale=T.cA[:, 1:2], bias=T.cA[:, 0:1]))
-    wait(S, s0)
-    s2 = one(S.activation(T.pA[:, :], T.tD[:, :], ACT.Abs, scale=-1.0, bias=T.cA[:, 3:4]))
-    add(s1, S.activation(T.cA[:, 4:5], T.cA[:, 1:2], ACT.Copy, scale=6.0 / 65536.0))
-    wait(S, s2)
-    s3 = one(S.activation(T.pP[:, :], T.pA[:, :], ACT.Relu, scale=-1.0, bias=T.kk[:, 1:2]))
-    add(s1, S.activation(T.cA[:, 5:6], T.cA[:, 1:2], ACT.Copy, scale=6.0))
-    wait(S, pb, ba)
-    bw = one(S.activation(T.bw[:, :], T.ps2[:, 0:32], ACT.Identity, bias=T.cA[:, 6:7]))
-    wait(S, s1, s3)
+    q3 = event()
+    add(q3, S.activation(T.cA[:, 24:26], cc, ACT.Sign, scale=-1.0, bias=T.kk[:, 8:9]))
+    add(q3, S.activation(T.cA[:, 26:28], cc, ACT.Abs, scale=-1.0, bias=T.kk[:, 2:3]))
+    add(q3, S.activation(T.cA[:, 28:30], cc, ACT.Sign, scale=-1.0, bias=T.kk[:, 2:3]))
+    wait(S, q3)
+    v2 = event()
+    add(v2, S.activation(T.cA[:, 6:8], T.cA[:, 24:26], ACT.Relu))
+    add(v2, S.activation(T.cA[:, 8:10], T.cA[:, 26:28], ACT.Relu, scale=-1.0, bias=T.kk[:, 1:2]))
+    add(v2, S.activation(T.cA[:, 10:12], T.cA[:, 28:30], ACT.Relu))
+    wait(S, pts[0])
+    iw = one(S.activation(T.IDW[:, w0:w1], T.ps3[:, :], ACT.Copy))
+    wait(S, iw, r1, d2, v2)
+    ii = event()
+    add(ii, S.activation(T.I1[:, :], T.IDW[:, w0:w1].indirect(T.R1[:, 0:1]), ACT.Copy, scale=T.cA[:, 7:8]))
+    add(ii, S.activation(T.I2[:, :], T.IDW[:, w0:w1].indirect(T.D2[:, 4 * rank:4 * rank + 4]), ACT.Copy, scale=T.cA[:, 6:7]))
+    wait(S, ii)
+    kt = event()
+    for j in range(4):
+        add(kt, S.activation(T.KT[:, t0 + 16 * j:t0 + 16 * j + 16], T.I2[:, 16 * j:16 * j + 16], ACT.Identity,
+                             bias=T.I1[:, 4 * rank + j:4 * rank + j + 1]))
+    wait(g, kt)
+    nK = send(T.KT[:, t0:t1], T.KT[:, t0:t1], T.sem.aK, T.sem.sK, others)
+    wait(g, iw)
+    nI = send(T.IDW[:, w0:w1], T.IDW[:, w0:w1], T.sem.aI, T.sem.sI, others)
+    pa = event()
+    add(pa, S.activation(T.pA[:, 0:64], T.tI[:, 0:64], ACT.Abs, bias=T.cA[:, 4:5]))
+    add(pa, S.activation(T.pA[:, 64:136], T.tI[:, 0:72], ACT.Abs, bias=T.cA[:, 4:5]))
+    q4 = event()
+    add(q4, S.activation(T.cA[:, 12:13], T.cA[:, 8:9], ACT.Identity, scale=65536.0, bias=T.cA[:, 10:11]))
+    add(q4, S.activation(T.cA[:, 13:14], T.cA[:, 9:10], ACT.Identity, scale=65536.0, bias=T.cA[:, 11:12]))
+    add(q4, S.activation(T.cA[:, 15:16], T.cA[:, 8:9], ACT.Copy, scale=393216.0))
+    add(q4, S.activation(T.cA[:, 16:17], T.cA[:, 8:9], ACT.Copy, scale=6.0))
+    sc = one(S.activation(T.cA[:, 18:24], T.kk[:, 0:6], ACT.Identity, scale=T.cA[:, 8:9], bias=T.kk[:, 1:2]))
+    wait(S, pa)
+    pp = one(S.activation(T.pP[:, :], T.pA[:, :], ACT.Relu, scale=-1.0, bias=T.kk[:, 1:2]))
+    wait(S, pp, q4)
     sel = event()
-    for k in range(1, 6):
-        add(sel, S.activation(T["D%d" % k][:, :], T.pP[:, :], ACT.Copy, scale=T.wk[:, k - 1:k]))
-    add(sel, S.activation(T.D6[:, 0:64], T.pP[:, 0:64], ACT.Copy, scale=T.cA[:, 5:6]))
-    add(sel, S.activation(T.D6[:, 64:136], T.pP[:, 64:136], ACT.Copy, scale=T.cA[:, 4:5]))
-    add(sel, S.activation(T.DI[:, :], T.pP[:, 64:136], ACT.Copy, scale=T.cA[:, 0:1]))
+    add(sel, S.activation(T.D[:, :], T.pP[:, :], ACT.Copy, scale=T.cA[:, 12:13]))
+    add(sel, S.activation(T.D1[:, :], T.pP[:, :], ACT.Copy, scale=T.cA[:, 13:14]))
+    add(sel, S.activation(T.D6[:, 0:64], T.pP[:, 0:64], ACT.Copy, scale=T.cA[:, 15:16]))
+    add(sel, S.activation(T.D6[:, 64:136], T.pP[:, 64:136], ACT.Copy, scale=T.cA[:, 16:17]))
+    add(sel, S.activation(T.DI[:, :], T.pP[:, 64:136], ACT.Copy, scale=T.cA[:, 10:11]))
 
-    S.wait_ge(T.sem.aI, nI * len(others))
-    wait(S, iw)
     bank = {1: T.ps4, 2: T.ps5, 3: T.ps6, 4: T.ps7, 5: T.ps3}
-    acc = [T.ps1, T.ps2]
-    gat, gid, idp, ky, ls = {}, {}, {}, {}, {(1, 0): l1, (1, 1): l1}
+    gat, gid, idp, ky = {}, {}, {}, {}
 
-    def idsum(out, m, D, k, bs):
+    def idsum(out, m, D, G, bs):
         for b in bs:
-            ins = P.matmul(out[0:m, 0:64], D[:, 7 - b:7 - b + m], T["G%d" % k][:, 64 * b:64 * b + 64], b == 0, b == 7)
+            ins = P.matmul(out[0:m, 0:64], D[:, 7 - b:7 - b + m], G[:, 64 * b:64 * b + 64], b == 0, b == 7)
         return ins
 
     def idstep(m):
-        wait(P, gid[m], sel)
+        k = max(m, 2)
+        wait(P, gid[k], sel)
         if m == 1:
-            wait(P, ohn)
-        idp[m] = one(idsum(bank[m], 128, T["D%d" % m], m, range(8)))
+            wait(P, ohn, we, wc)
+        idp[m] = one(idsum(bank[m], 128, T.D1 if m == 1 else T.D, T["G%d" % k], range(8)))
 
     def keystep(k):
         wait(V, idp[k])
@@ -296,46 +329,62 @@ def rank_program(g, core, T, topo):
             ky[k] = one(V.tensor_tensor(o[:, :], T.key[:, :], bank[k][:, 0:64], A.max))
 
     def gather(k, s):
-        c = 32 * k - 64 + 16 * s
+        c = 32 * k - 96 + 16 * s
         wait(V, ls[k - 1, s])
-        gat[k, s] = one(V.tensor_tensor(T["RM%d" % s][:, :], T.W[:, :].indirect(T.LS[:, c:c + 16]),
+        gat[k, s] = one(V.tensor_tensor(T["RM%d" % s][:, :], (T.T3 if k == 3 else T.W)[:, :].indirect(T.LS[:, c:c + 16]),
                                         T.OH[:, 256 * s + k - 1:256 * s + k + 255], A.mult))
 
     def idgather(k):
         wait(S, ls[k, 0], ls[k, 1])
-        gid[k] = one(S.activation(T["G%d" % k][:, :], T.IDW[:, :].indirect(T.LS[:, 32 * k - 32:32 * k]), ACT.Copy))
+        gid[k] = one(S.activation(T["G%d" % k][:, :], (T.KT if k == 2 else T.IDW)[:, :].indirect(T.LS[:, 32 * k - 64:32 * k - 32]),
+                                  ACT.Copy, scale=T.cA[:, 17 + k:18 + k]))
 
-    idgather(1)
-    for h in range(2):
-        V.wait_ge(T.sem["aW%d" % h], nW * len(others))
-    wait(V, wcs[0], wcs[1], oh)
-    gather(2, 0)
-    wait(V, ohn)
-    gather(2, 1)
-    wait(P, bw)
-    begin = {4: 1, 5: 2, 6: 3}
-    keys = {(4, 1): 1, (5, 1): 2, (6, 0): 3, (6, 1): 4}
-    for k in range(2, 7):
-        if k in begin:
-            idstep(begin[k])
+    V.wait_ge(T.sem.aT, nT * len(others))
+    wait(V, t3, oa)
+    gather(3, 0)
+    wait(V, pairs1)
+    copylist(2, 1)
+    wait(V, ob, ohn)
+    gather(3, 1)
+    ident = one(V.tensor_scalar(T.ID[:, :], T.tI[:, 15:143], pcol, None, A.is_equal))
+    wait(V, ls[2, 0], ls[2, 1])
+    li = one(V.tensor_copy(T.LI[:, :], T.LS[:, 0:32]))
+    wait(V, li)
+    lo = one(V.tensor_scalar(T.LO[:, :], T.LI[:, :], 6, None, A.arith_shift_right))
+    wait(V, lo)
+    bw = one(V.tensor_scalar(T.bw[:, :], T.LO[:, :], 512.0, 256.0, A.mult, A.add))
+    S.wait_ge(T.sem.aK, nK * len(others))
+    wait(S, sc, kt)
+    idgather(2)
+    S.wait_ge(T.sem.aI, nI * len(others))
+    wait(P, bs)
+    begin = {(5, 1): 1, (6, 0): 2, (6, 1): 3}
+    keys = {(5, 1): (1,), (6, 0): (2,), (6, 1): (3, 4)}
+    for k in range(3, 7):
         pm = []
         for s in range(2):
+            if (k, s) in begin:
+                idstep(begin[k, s])
             wait(P, ls[k - 1, s])
-            P.matmul(acc[s][:, 0:16], T.ID[:, :], T.bw[:, 16 * s:16 * s + 16], True, False)
+            if k > 3:
+                wait(P, bw, ident)
+                P.matmul(acc[s][:, 0:16], T.ID[:, :], T.bw[:, 16 * s:16 * s + 16], True, False)
             wait(P, gat[k, s])
             for x in range(16):
-                ins = P.matmul(acc[s][:, 0:16], T.B[:, 15 - x:143 - x], T["RM%d" % s][:, x:256:16], False, x == 15)
+                ins = P.matmul(acc[s][:, 0:16], T.B[:, 15 - x:143 - x], T["RM%d" % s][:, x:256:16], k == 3 and x == 0, x == 15)
             pm.append(one(ins))
         if k == 6:
             idstep(4)
             idstep(5)
         for s in range(2):
-            c = 32 * k - 32 + 16 * s
+            c = 32 * k - 64 + 16 * s
             wait(V, pm[s])
-            ls[k, s] = one(V.tensor_copy(T.LS[:, c:c + 16], acc[s][:, 0:16]))
-            if (k, s) in keys:
-                keystep(keys[k, s])
+            copylist(k, s)
+            for m in keys.get((k, s), ()):
+                keystep(m)
             if k < 6:
+                if k == 3 and s == 0:
+                    V.wait_ge(T.sem.aW, nW * len(others))
                 gather(k + 1, s)
             elif s == 0:
                 V.wait_ge(T.sem.aI, nI * len(others))
@@ -350,11 +399,11 @@ def rank_program(g, core, T, topo):
             idgather(k)
     zb, ib = T.ps0, T.ps1
     wait(P, i0)
-    idsum(zb, 128, T.D6, 6, range(4))
-    idsum(ib, 64, T.DI, 6, range(4))
+    idsum(zb, 128, T.D6, T.G6, range(4))
+    idsum(ib, 64, T.DI, T.G6, range(4))
     wait(P, i1, i2)
-    pz = one(idsum(zb, 128, T.D6, 6, range(4, 8)))
-    pi = one(idsum(ib, 64, T.DI, 6, range(4, 8)))
+    pz = one(idsum(zb, 128, T.D6, T.G6, range(4, 8)))
+    pi = one(idsum(ib, 64, T.DI, T.G6, range(4, 8)))
     keystep(5)
     wait(V, ky[5])
     k5 = event()
@@ -370,9 +419,10 @@ def rank_program(g, core, T, topo):
     wait(Y, od)
     Y.dma_start(T.yid[:, :], T.OD[0:64, :]).then_inc(T.sem.oY, 16)
     g.wait_ge(T.sem.sH, nH)
-    g.wait_ge(T.sem.sW0, nW)
-    g.wait_ge(T.sem.sW1, nW)
+    g.wait_ge(T.sem.sT, nT)
+    g.wait_ge(T.sem.sW, nW)
     g.wait_ge(T.sem.sI, nI)
+    g.wait_ge(T.sem.sK, nK)
     for e in evs:
         if not e[2]:
             wait(g, e)

@@ -9,7 +9,7 @@ SCRATCH = {
     "I64": ("sbuf", [128, 64], "bfloat16"),
     "W": ("sbuf", [128, 2048], "bfloat16"),
     "IDW": ("sbuf", [128, 2048], "bfloat16"),
-    "T3": ("sbuf", [128, 256], "float32"),
+    "T3": ("sbuf", [128, 256], "bfloat16"),
     "KT": ("sbuf", [128, 256], "bfloat16"),
     "R1": ("sbuf", [128, 2], "uint16"),
     "D2": ("sbuf", [128, 16], "uint16"),
@@ -20,28 +20,23 @@ SCRATCH = {
     "L4h": ("sbuf", [128, 128], "bfloat16"),
     "Lnh": ("sbuf", [128, 8], "bfloat16"),
     "T4": ("sbuf", [128, 128], "int32"),
-    "T4f": ("sbuf", [128, 128], "float32"),
     "X4": ("sbuf", [128, 128], "bfloat16"),
     "OH": ("sbuf", [128, 528], "bfloat16"),
-    "RM0": ("sbuf", [128, 256], "float16"),
-    "RM1": ("sbuf", [128, 256], "float16"),
+    "RM0": ("sbuf", [128, 256], "bfloat16"),
+    "RM1": ("sbuf", [128, 256], "bfloat16"),
     "LS": ("sbuf", [128, 160], "uint16"),
-    "LI": ("sbuf", [128, 32], "int32"),
-    "LO": ("sbuf", [128, 32], "int32"),
     "cI": ("sbuf", [128, 6], "int32"),
     "cF": ("sbuf", [128, 6], "float32"),
     "cA": ("sbuf", [128, 32], "float32"),
     "tI": ("sbuf", [128, 144], "bfloat16"),
     "pL": ("sbuf", [128, 144], "float32"),
-    "pM": ("sbuf", [128, 144], "float32"),
     "pA": ("sbuf", [128, 136], "float32"),
     "pP": ("sbuf", [128, 136], "float32"),
     "eR": ("sbuf", [128, 128], "bfloat16"),
     "eE": ("sbuf", [128, 128], "bfloat16"),
     "RQ": ("sbuf", [128, 512], "bfloat16"),
     "EQ": ("sbuf", [128, 512], "bfloat16"),
-    "kk": ("sbuf", [128, 10], "float32"),
-    "B": ("sbuf", [128, 144], "float16"),
+    "B": ("sbuf", [128, 144], "bfloat16"),
     "BL": ("sbuf", [128, 144], "bfloat16"),
     "BC": ("sbuf", [128, 144], "bfloat16"),
     "BD": ("sbuf", [128, 144], "bfloat16"),
@@ -116,9 +111,9 @@ def rank_program(g, core, T, topo):
     def kid(q, j):
         q.dma_start(T.KR[:, j, :, :], T.kid[j:8:4, :]).then_inc(T.sem["lK%d" % j], 16)
 
+    S.dma_start(T.L4[0:32, :], T.lett[:, :]).then_inc(T.sem.lL, 16)
     kid(Y, 0)
     kid(S, 1)
-    S.dma_start(T.L4[0:32, :], T.lett[:, :]).then_inc(T.sem.lL, 16)
     kid(Y, 2)
     kid(Y, 3)
     for j in range(3):
@@ -126,16 +121,19 @@ def rank_program(g, core, T, topo):
 
     imp = {"allow_small_or_imprecise_dtypes": True}
     c0 = one(g.iota(T.cI[:, 0:2], [[8, 2]], 0, 1))
-    c1 = one(g.iota(T.tI[:, :], [[1, 144]], -15, 0, **imp))
-    ck = one(g.iota(T.kk[:, :], [[1, 10]], 0, 0, **imp))
     c2 = one(g.iota(T.eR[0:32, :], [[4, 8], [0, 16]], 0, -1, **imp))
+    c1 = one(g.iota(T.tI[:, :], [[1, 144]], -15, 0, **imp))
+    c3 = one(g.iota(T.eE[0:96, :], [[4, 8], [0, 2], [32, 8]], 0, -1, **imp))
+
+    def num(j):
+        return T.tI[:, 15 + j:16 + j]
+
     v0 = event()
     add(v0, V.memset(T.L4[32:64, 0:8], 0))
     add(v0, V.memset(T.L4[64:128, 0:8], 0))
     wait(g, v0)
     g.wait_ge(T.sem.lL, 16)
     nH = send(T.LN[:, 0:8], T.L4[:, 0:8], T.sem.aH, T.sem.sH, [T.cores[(rank + n - 1) % n]])
-    c3 = one(g.iota(T.eE[0:96, :], [[4, 8], [0, 2], [32, 8]], 0, -1, **imp))
 
     wait(V, c0)
     v1 = event()
@@ -146,132 +144,142 @@ def rank_program(g, core, T, topo):
     cf = one(V.tensor_copy(T.cF[:, :], T.cI[:, :]))
     pcol, ccol, ycol, s16 = [T.cF[:, j:j + 1] for j in (0, 2, 4, 5)]
     cc = T.cF[:, 2:4]
-    wait(V, cf, c1)
-    i64 = one(V.tensor_scalar(T.I64[:, :], T.tI[:, 15:79], ycol, None, A.is_equal))
 
-    wait(S, ck, cf)
+    wait(S, c1, cf)
     q0 = event()
     add(q0, S.activation(T.cA[:, 0:1], ccol, ACT.Copy, scale=17.0))
     add(q0, S.activation(T.cA[:, 1:2], ccol, ACT.Copy, scale=-1.0))
-    add(q0, S.activation(T.cA[:, 3:4], s16, ACT.Identity, scale=-17.0, bias=T.kk[:, 1:2]))
+    add(q0, S.activation(T.cA[:, 3:4], s16, ACT.Identity, scale=-17.0, bias=num(1)))
     add(q0, S.activation(T.cA[:, 2:3], ccol, ACT.Copy, scale=16.0))
-    wait(S, q0, c1)
+    wait(S, q0)
     ql = one(S.activation(T.pL[:, :], T.tI[:, :], ACT.Abs, scale=17.0, bias=T.cA[:, 3:4]))
     wait(S, ql)
     bl = one(S.activation(T.BL[:, :], T.pL[:, :], ACT.Relu, scale=T.cA[:, 1:2], bias=T.cA[:, 0:1]))
 
+    wait(V, c2)
+    sr = event()
+    for q in range(4):
+        add(sr, V.tensor_scalar(T.RQ[0:32, 128 * q:128 * q + 128], T.eR[0:32, :], float(-q), None, A.is_equal))
+    V.wait_ge(T.sem.lL, 16)
+    lr = one(V.tensor_copy(T.L4h[0:32, :], T.L4[0:32, :]))
+    wait(P, lr, sr)
+    for q in range(4):
+        ins = P.matmul(T.ps0[:, 128 * q:128 * q + 128], T.RQ[0:32, 128 * q:128 * q + 128], T.L4h[0:32, :], True, True)
+    pl = one(ins)
+
+    wait(V, cf, c1)
+    i64 = one(V.tensor_scalar(T.I64[:, :], T.tI[:, 15:79], ycol, None, A.is_equal))
     cvs = []
     for j in range(4):
         V.wait_ge(T.sem["lK%d" % j], 16)
         cvs.append(one(V.tensor_scalar(T.KB[:, :, 16 * j:16 * j + 16], T.KR[:, j, :, :], -256.0, None, A.add)))
     wait(P, i64, *cvs)
-    tr = []
-    for h, out in ((0, T.ps5), (1, T.ps7)):
-        for b in range(h, R, 2):
+    tr = {}
+    tb = {0: T.ps5, 2: T.ps7, 1: T.ps6, 3: T.ps4}
+    for h in (0, 2, 1, 3):
+        for b in (h, h + 4):
             for a in (0, 64):
-                ins = P.matmul(out[a:a + 64, b // 2:256:R // 2], T.KB[a:a + 64, b, :], T.I64[a:a + 64, :], True, True)
-        tr.append(one(ins))
-    wait(S, tr[0])
-    we = one(S.activation(T.W[:, w0:w1:2], T.ps5[:, 0:256], ACT.Copy))
-    V.wait_ge(T.sem.lL, 16)
-    lr = one(V.tensor_copy(T.L4h[0:32, :], T.L4[0:32, :]))
-    wait(V, c2)
-    sr = event()
-    for q in range(4):
-        add(sr, V.tensor_scalar(T.RQ[0:32, 128 * q:128 * q + 128], T.eR[0:32, :], float(-q), None, A.is_equal))
+                ins = P.matmul(tb[h][a:a + 64, b // 4:128:2], T.KB[a:a + 64, b, :], T.I64[a:a + 64, :], True, True)
+        tr[h] = one(ins)
     V.wait_ge(T.sem.lT, 48)
-    tf = one(V.tensor_copy(T.T4f[0:96, :], T.T4[0:96, :]))
-    wait(P, lr, sr)
-    for q in range(4):
-        ins = P.matmul(T.ps0[:, 128 * q:128 * q + 128], T.RQ[0:32, 128 * q:128 * q + 128], T.L4h[0:32, :], True, True)
-    pl = one(ins)
+    tf = one(V.tensor_copy(T.ps3[0:96, 0:128], T.T4[0:96, :]))
+    wait(V, pl)
+    oa = one(V.tensor_scalar(T.OH[:, 0:272], T.ps0[:, 0:272], ccol, None, A.is_equal))
+    bs = one(V.tensor_scalar(T.B[:, :], T.tI[:, :], s16, None, A.is_equal))
+    se = []
+
+    def selectors(h):
+        wait(V, c3)
+        e = event()
+        for q in (2 * h, 2 * h + 1):
+            add(e, V.tensor_scalar(T.EQ[0:96, 128 * q:128 * q + 128], T.eE[0:96, :], float(-q), None, A.is_equal))
+        se.append(e)
+
+    selectors(0)
+    we = event()
+    for h in (0, 2, 3):
+        if h == 3:
+            wait(S, tf)
+            hp = one(S.activation(T.X4[0:96, :], T.ps3[0:96, 0:128], ACT.Copy))
+        wait(S, tr[h])
+        add(we, S.activation(T.W[:, w0 + h:w1:4], tb[h][:, 0:128], ACT.Copy))
+    wait(S, hp)
+    fp = one(S.activation(T.X4[64:96, :], T.X4[64:96, :], ACT.Sign))
+    wait(S, bs, q0)
+    bc = event()
+    add(bc, S.activation(T.BC[:, :], T.B[:, :], ACT.Copy, scale=ccol))
+    add(bc, S.activation(T.BD[:, :], T.B[:, :], ACT.Copy, scale=T.cA[:, 2:3]))
     wait(V, tr[1])
-    r1 = one(V.tensor_scalar(T.R1[:, 0:1], T.ps7[:, 0:1], 256.0, None, A.add))
-    wc = one(V.tensor_copy(T.W[:, w0 + 1:w1:2], T.ps7[:, 0:256]))
+    r1 = one(V.tensor_scalar(T.R1[:, 0:1], tb[1][:, 0:1], 256.0, None, A.add))
+    wc = one(V.tensor_copy(T.W[:, w0 + 1:w1:4], tb[1][:, 0:128]))
+    wait(V, hp, tf)
+    qp = one(V.tensor_tensor(T.X4[32:64, :], T.ps3[32:64, 0:128], T.X4[32:64, :], A.subtract))
     wait(V, r1, we, wc)
     d2 = one(V.tensor_scalar(T.D2[:, :], T.W[:, w0:w1].indirect(T.R1[:, 0:1]), 256.0, None, A.add))
+    v2 = one(V.tensor_scalar(T.cA[:, 6:8], cc, 8.0, None, A.is_lt))
     wait(V, d2)
-    t3 = one(V.tensor_scalar(T.T3[:, t0:t1], T.W[:, w0:w1].indirect(T.D2[:, 4 * rank:4 * rank + 4]), 256.0 + w0, None, A.add))
+    t3 = one(V.tensor_copy(T.T3[:, t0:t1], T.W[:, w0:w1].indirect(T.D2[:, 4 * rank:4 * rank + 4])))
     wait(g, t3)
     nT = send(T.T3[:, t0:t1], T.T3[:, t0:t1], T.sem.aT, T.sem.sT, others)
     wait(g, we, wc)
     nW = send(T.W[:, w0:w1], T.W[:, w0:w1], T.sem.aW, T.sem.sW, others)
 
-    wait(S, tf)
-    hp = one(S.activation(T.X4[0:64, :], T.T4f[0:64, :], ACT.Copy))
-    fp = one(S.activation(T.X4[64:96, :], T.T4f[64:96, :], ACT.Sign))
-    q1 = event()
-    add(q1, S.activation(T.cA[:, 5:6], s16, ACT.Copy, scale=-1.0))
-    add(q1, S.activation(T.cA[:, 14:15], ccol, ACT.Copy, scale=-16.0))
-    add(q1, S.activation(T.cA[:, 4:5], s16, ACT.Identity, scale=-0.5, bias=T.kk[:, 8:9]))
-    wait(S, q1)
-    q2 = one(S.activation(T.pM[:, :], T.tI[:, :], ACT.Abs, bias=T.cA[:, 5:6]))
-    wait(S, q2)
-    bc = event()
-    add(bc, S.activation(T.BC[:, :], T.pM[:, :], ACT.Relu, scale=T.cA[:, 1:2], bias=ccol))
-    add(bc, S.activation(T.BD[:, :], T.pM[:, :], ACT.Relu, scale=T.cA[:, 14:15], bias=T.cA[:, 2:3]))
-
-    wait(V, pl)
-    oa = one(V.tensor_scalar(T.OH[:, 0:272], T.ps0[:, 0:272], ccol, None, A.is_equal))
-    wait(V, c3)
-    se = event()
-    for q in range(4):
-        add(se, V.tensor_scalar(T.EQ[0:96, 128 * q:128 * q + 128], T.eE[0:96, :], float(-q), None, A.is_equal))
-    wait(V, hp, tf)
-    qp = one(V.tensor_tensor(T.X4[32:64, :], T.T4f[32:64, :], T.X4[32:64, :], A.subtract))
+    selectors(1)
     ob = one(V.tensor_scalar(T.OH[:, 272:512], T.ps0[:, 272:512], ccol, None, A.is_equal))
     V.wait_ge(T.sem.aH, nH)
     ln = one(V.tensor_copy(T.Lnh[0:32, :], T.LN[0:32, :]))
-    bs = one(V.tensor_scalar(T.B[:, :], T.tI[:, :], s16, None, A.is_equal))
-
     acc = [T.ps1, T.ps2]
-    pts = []
-
-    def ids():
-        wait(P, se, hp, fp, qp)
-        for q in range(4):
-            ins = P.matmul(T.ps3[:, 128 * q:128 * q + 128], T.EQ[0:96, 128 * q:128 * q + 128], T.X4[0:96, :], True, True)
-        pts.append(one(ins))
 
     def pairs(s):
         a = 256 * s
         for x in range(1, 16):
             P.matmul(acc[s][:, 0:16], T.BL[:, 15 - x:143 - x], T.OH[:, a + x:a + 256:16], x == 1, False)
-        if s == 0:
-            ids()
         wait(P, bc)
         P.matmul(acc[s][:, 0:16], T.BD[:, 15:143], T.OH[:, a:a + 256:16], False, False)
         return one(P.matmul(acc[s][:, 0:16], T.BC[:, 0:128], T.OH[:, a + 16:a + 257:16], False, True))
 
     wait(P, oa, bl)
     pairs0 = pairs(0)
+    wait(P, hp, fp, qp, we)
+    ti, pt = [T.ps5, T.ps3], []
+    for h in range(2):
+        wait(P, se[h])
+        for q in range(2):
+            c = 256 * h + 128 * q
+            ins = P.matmul(ti[h][:, 128 * q:128 * q + 128], T.EQ[0:96, c:c + 128], T.X4[0:96, :], True, True)
+        pt.append(one(ins))
     wait(P, ln)
-    ph = one(P.matmul(T.ps4[:, 0:8], T.RQ[0:32, 0:128], T.Lnh[0:32, :], True, True))
+    ph = one(P.matmul(T.ps4[:, 256:264], T.RQ[0:32, 0:128], T.Lnh[0:32, :], True, True))
 
-    ls = {}
+    ls, bw = {}, {}
 
     def copylist(k, s):
         c = 32 * k - 64 + 16 * s
-        ls[k, s] = one(V.tensor_copy(T.LS[:, c:c + 16], acc[s][:, 0:16]))
+        if k == 2:
+            ls[k, s] = one(V.tensor_copy(T.LS[:, c:c + 16], acc[s][:, 0:16]))
+        else:
+            ls[k, s] = one(V.tensor_scalar(T.LS[:, c:c + 16], acc[s][:, 0:16], 256.0 - 66048.0, None, A.add))
+
+    def owners(s):
+        wait(V, ls[2, s])
+        bw[s] = one(V.tensor_scalar(T.bw[:, 16 * s:16 * s + 16], T.LS[:, 16 * s:16 * s + 16], 8224.5, None, A.add))
 
     wait(V, pairs0)
     copylist(2, 0)
+    ident = one(V.tensor_scalar(T.ID[:, :], T.tI[:, 15:143], pcol, 8.0, A.is_equal, A.mult))
+    owners(0)
     wait(V, ph)
-    ohn = one(V.tensor_scalar(T.OH[:, 512:520], T.ps4[:, 0:8], ccol, None, A.is_equal))
+    ohn = one(V.tensor_scalar(T.OH[:, 512:520], T.ps4[:, 256:264], ccol, None, A.is_equal))
     wait(P, ob, ohn)
     pairs1 = pairs(1)
+    v3 = event()
+    add(v3, V.tensor_scalar(T.cA[:, 8:10], cc, 2.0, None, A.is_equal))
+    add(v3, V.tensor_scalar(T.cA[:, 10:12], cc, 2.0, None, A.is_lt))
 
-    q3 = event()
-    add(q3, S.activation(T.cA[:, 24:26], cc, ACT.Sign, scale=-1.0, bias=T.kk[:, 8:9]))
-    add(q3, S.activation(T.cA[:, 26:28], cc, ACT.Abs, scale=-1.0, bias=T.kk[:, 2:3]))
-    add(q3, S.activation(T.cA[:, 28:30], cc, ACT.Sign, scale=-1.0, bias=T.kk[:, 2:3]))
-    wait(S, q3)
-    v2 = event()
-    add(v2, S.activation(T.cA[:, 6:8], T.cA[:, 24:26], ACT.Relu))
-    add(v2, S.activation(T.cA[:, 8:10], T.cA[:, 26:28], ACT.Relu, scale=-1.0, bias=T.kk[:, 1:2]))
-    add(v2, S.activation(T.cA[:, 10:12], T.cA[:, 28:30], ACT.Relu))
-    wait(S, pts[0])
-    iw = one(S.activation(T.IDW[:, w0:w1], T.ps3[:, :], ACT.Copy))
+    iw = event()
+    for h in range(2):
+        wait(S, pt[h])
+        add(iw, S.activation(T.IDW[:, w0 + 256 * h:w0 + 256 * h + 256], ti[h][:, 0:256], ACT.Copy))
     wait(S, iw, r1, d2, v2)
     ii = event()
     add(ii, S.activation(T.I1[:, :], T.IDW[:, w0:w1].indirect(T.R1[:, 0:1]), ACT.Copy, scale=T.cA[:, 7:8]))
@@ -285,6 +293,8 @@ def rank_program(g, core, T, topo):
     nK = send(T.KT[:, t0:t1], T.KT[:, t0:t1], T.sem.aK, T.sem.sK, others)
     wait(g, iw)
     nI = send(T.IDW[:, w0:w1], T.IDW[:, w0:w1], T.sem.aI, T.sem.sI, others)
+    q1 = one(S.activation(T.cA[:, 4:5], s16, ACT.Identity, scale=-0.5, bias=num(8)))
+    wait(S, q1, v3)
     pa = event()
     add(pa, S.activation(T.pA[:, 0:64], T.tI[:, 0:64], ACT.Abs, bias=T.cA[:, 4:5]))
     add(pa, S.activation(T.pA[:, 64:136], T.tI[:, 0:72], ACT.Abs, bias=T.cA[:, 4:5]))
@@ -293,9 +303,9 @@ def rank_program(g, core, T, topo):
     add(q4, S.activation(T.cA[:, 13:14], T.cA[:, 9:10], ACT.Identity, scale=65536.0, bias=T.cA[:, 11:12]))
     add(q4, S.activation(T.cA[:, 15:16], T.cA[:, 8:9], ACT.Copy, scale=393216.0))
     add(q4, S.activation(T.cA[:, 16:17], T.cA[:, 8:9], ACT.Copy, scale=6.0))
-    sc = one(S.activation(T.cA[:, 18:24], T.kk[:, 0:6], ACT.Identity, scale=T.cA[:, 8:9], bias=T.kk[:, 1:2]))
+    sc = one(S.activation(T.cA[:, 18:24], T.tI[:, 15:21], ACT.Identity, scale=T.cA[:, 8:9], bias=num(1)))
     wait(S, pa)
-    pp = one(S.activation(T.pP[:, :], T.pA[:, :], ACT.Relu, scale=-1.0, bias=T.kk[:, 1:2]))
+    pp = one(S.activation(T.pP[:, :], T.pA[:, :], ACT.Relu, scale=-1.0, bias=num(1)))
     wait(S, pp, q4)
     sel = event()
     add(sel, S.activation(T.D[:, :], T.pP[:, :], ACT.Copy, scale=T.cA[:, 12:13]))
@@ -316,7 +326,7 @@ def rank_program(g, core, T, topo):
         k = max(m, 2)
         wait(P, gid[k], sel)
         if m == 1:
-            wait(P, ohn, we, wc)
+            wait(P, ohn, r1, we, wc, iw)
         idp[m] = one(idsum(bank[m], 128, T.D1 if m == 1 else T.D, T["G%d" % k], range(8)))
 
     def keystep(k):
@@ -339,6 +349,11 @@ def rank_program(g, core, T, topo):
         gid[k] = one(S.activation(T["G%d" % k][:, :], (T.KT if k == 2 else T.IDW)[:, :].indirect(T.LS[:, 32 * k - 64:32 * k - 32]),
                                   ACT.Copy, scale=T.cA[:, 17 + k:18 + k]))
 
+    def addowners(s, start, stop):
+        if start is not stop and stop:
+            wait(P, bw[s], ident)
+        return P.matmul(acc[s][:, 0:16], T.ID[:, :], T.bw[:, 16 * s:16 * s + 16], start, stop)
+
     V.wait_ge(T.sem.aT, nT * len(others))
     wait(V, t3, oa)
     gather(3, 0)
@@ -346,20 +361,14 @@ def rank_program(g, core, T, topo):
     copylist(2, 1)
     wait(V, ob, ohn)
     gather(3, 1)
-    ident = one(V.tensor_scalar(T.ID[:, :], T.tI[:, 15:143], pcol, None, A.is_equal))
-    wait(V, ls[2, 0], ls[2, 1])
-    li = one(V.tensor_copy(T.LI[:, :], T.LS[:, 0:32]))
-    wait(V, li)
-    lo = one(V.tensor_scalar(T.LO[:, :], T.LI[:, :], 6, None, A.arith_shift_right))
-    wait(V, lo)
-    bw = one(V.tensor_scalar(T.bw[:, :], T.LO[:, :], 512.0, 256.0, A.mult, A.add))
+    owners(1)
     S.wait_ge(T.sem.aK, nK * len(others))
     wait(S, sc, kt)
     idgather(2)
     S.wait_ge(T.sem.aI, nI * len(others))
     wait(P, bs)
-    begin = {(5, 1): 1, (6, 0): 2, (6, 1): 3}
-    keys = {(5, 1): (1,), (6, 0): (2,), (6, 1): (3, 4)}
+    begin = {(5, 0): 1, (5, 1): 2, (6, 1): 3}
+    keys = {(5, 1): 1, (6, 0): 2, (6, 1): 3}
     for k in range(3, 7):
         pm = []
         for s in range(2):
@@ -367,11 +376,13 @@ def rank_program(g, core, T, topo):
                 idstep(begin[k, s])
             wait(P, ls[k - 1, s])
             if k > 3:
-                wait(P, bw, ident)
-                P.matmul(acc[s][:, 0:16], T.ID[:, :], T.bw[:, 16 * s:16 * s + 16], True, False)
+                addowners(s, True, False)
             wait(P, gat[k, s])
             for x in range(16):
-                ins = P.matmul(acc[s][:, 0:16], T.B[:, 15 - x:143 - x], T["RM%d" % s][:, x:256:16], k == 3 and x == 0, x == 15)
+                ins = P.matmul(acc[s][:, 0:16], T.B[:, 15 - x:143 - x], T["RM%d" % s][:, x:256:16],
+                               k == 3 and x == 0, k > 3 and x == 15)
+            if k == 3:
+                ins = addowners(s, False, True)
             pm.append(one(ins))
         if k == 6:
             idstep(4)
@@ -380,8 +391,8 @@ def rank_program(g, core, T, topo):
             c = 32 * k - 64 + 16 * s
             wait(V, pm[s])
             copylist(k, s)
-            for m in keys.get((k, s), ()):
-                keystep(m)
+            if (k, s) in keys:
+                keystep(keys[k, s])
             if k < 6:
                 if k == 3 and s == 0:
                     V.wait_ge(T.sem.aW, nW * len(others))
@@ -404,6 +415,7 @@ def rank_program(g, core, T, topo):
     wait(P, i1, i2)
     pz = one(idsum(zb, 128, T.D6, T.G6, range(4, 8)))
     pi = one(idsum(ib, 64, T.DI, T.G6, range(4, 8)))
+    keystep(4)
     keystep(5)
     wait(V, ky[5])
     k5 = event()

from concourse.bass import DstId, RemoteDMATransfer
from concourse.mybir import AluOpType, ActivationFunctionType

R = 8

SCRATCH = {
    "KR": ("sbuf", [128, 4, R, 16], "int32"),
    "KB": ("sbuf", [128, R, 64], "bfloat16"),
    "I64": ("sbuf", [128, 64], "bfloat16"),
    "W": ("sbuf", [128, 2048], "bfloat16"),
    "IDW": ("sbuf", [128, 2048], "bfloat16"),
    "T3": ("sbuf", [128, 256], "bfloat16"),
    "KT": ("sbuf", [128, 256], "bfloat16"),
    "R1": ("sbuf", [128, 2], "uint16"),
    "D2": ("sbuf", [128, 16], "uint16"),
    "I1": ("sbuf", [128, 16], "float32"),
    "I2": ("sbuf", [128, 64], "bfloat16"),
    "L4": ("sbuf", [128, 128], "int32"),
    "LN": ("sbuf", [128, 8], "int32"),
    "L4h": ("sbuf", [128, 128], "bfloat16"),
    "Lnh": ("sbuf", [128, 8], "bfloat16"),
    "T4": ("sbuf", [128, 128], "int32"),
    "X4": ("sbuf", [128, 128], "bfloat16"),
    "OH": ("sbuf", [128, 528], "bfloat16"),
    "RM0": ("sbuf", [128, 256], "bfloat16"),
    "RM1": ("sbuf", [128, 256], "bfloat16"),
    "LS": ("sbuf", [128, 160], "uint16"),
    "cI": ("sbuf", [128, 6], "int32"),
    "cF": ("sbuf", [128, 6], "float32"),
    "cA": ("sbuf", [128, 32], "float32"),
    "tI": ("sbuf", [128, 144], "bfloat16"),
    "pL": ("sbuf", [128, 144], "float32"),
    "pA": ("sbuf", [128, 136], "float32"),
    "pP": ("sbuf", [128, 136], "float32"),
    "eR": ("sbuf", [128, 128], "bfloat16"),
    "eE": ("sbuf", [128, 128], "bfloat16"),
    "RQ": ("sbuf", [128, 512], "bfloat16"),
    "EQ": ("sbuf", [128, 512], "bfloat16"),
    "B": ("sbuf", [128, 144], "bfloat16"),
    "BL": ("sbuf", [128, 144], "bfloat16"),
    "BC": ("sbuf", [128, 144], "bfloat16"),
    "BD": ("sbuf", [128, 144], "bfloat16"),
    "ID": ("sbuf", [128, 128], "bfloat16"),
    "bw": ("sbuf", [128, 32], "bfloat16"),
    "D": ("sbuf", [128, 136], "bfloat16"),
    "D1": ("sbuf", [128, 136], "bfloat16"),
    "D6": ("sbuf", [128, 136], "bfloat16"),
    "DI": ("sbuf", [128, 72], "bfloat16"),
    "key": ("sbuf", [128, 64], "float32"),
    "keyI": ("sbuf", [128, 64], "int32"),
    "idI": ("sbuf", [128, 64], "int32"),
    "kI": ("sbuf", [128, 64], "int32"),
    "u": ("sbuf", [128, 64], "float32"),
    "OL": ("sbuf", [128, 64], "float32"),
    "OD": ("sbuf", [128, 64], "float32"),
}
for _k in range(2, 7):
    SCRATCH["G%d" % _k] = ("sbuf", [128, 512], "bfloat16")
for _k in range(8):
    SCRATCH["ps%d" % _k] = ("psum", [128, 512], "float32")

SEMAPHORES = ["lL", "lT", "lK0", "lK1", "lK2", "lK3", "aH", "aT", "aW", "aI", "aK", "sH", "sT", "sW", "sI", "sK", "oY"] + ["e%d" % k for k in range(130)]


def rank_program(g, core, T, topo):
    rank = T.rank_of(core)
    if rank is None:
        return
    A, ACT = AluOpType, ActivationFunctionType
    V, S, P, Y = g.vector, g.scalar, g.tensor, g.sync
    n = len(T.cores)
    others = [T.cores[(rank + d) % n] for d in range(1, n)]
    used = [0]
    evs = []

    def event():
        e = [T.sem["e%d" % used[0]], 0, 0]
        used[0] += 1
        evs.append(e)
        return e

    def add(e, ins):
        e[1] += 1
        ins.then_inc(e[0], 1)

    def one(ins):
        e = event()
        add(e, ins)
        return e

    def wait(q, *es):
        for e in es:
            q.wait_ge(e[0], e[1])
            e[2] = 1

    def send(dst, src, rsem, lsem, cores):
        m = topo.mask(core, cores[0])
        for d in cores:
            m &= topo.mask(core, d)
        ids = []
        for d in cores:
            a = topo.addr(d)
            ids.append(DstId(rid=a[0], pnc=a[1]))
        g.remote_dma_fused([RemoteDMATransfer(dst_ids=ids, dma_engine_mask=m, remote_sem=rsem, srcs=[src],
                                              dsts=[dst for d in cores])], local_sem=lsem)
        return bin(m).count("1")

    w0, w1 = 512 * rank, 512 * rank + 512
    t0, t1 = 64 * rank, 64 * rank + 64

    def kid(q, j):
        q.dma_start(T.KR[:, j, :, :], T.kid[j:8:4, :]).then_inc(T.sem["lK%d" % j], 16)

    S.dma_start(T.L4[0:32, :], T.lett[:, :]).then_inc(T.sem.lL, 16)
    kid(Y, 0)
    kid(S, 1)
    kid(Y, 2)
    kid(Y, 3)
    for j in range(3):
        Y.dma_start(T.T4[32 * j:32 * j + 32, :], T.tid[:, :]).then_inc(T.sem.lT, 16)

    imp = {"allow_small_or_imprecise_dtypes": True}
    c0 = one(g.iota(T.cI[:, 0:2], [[8, 2]], 0, 1))
    c2 = one(g.iota(T.eR[0:32, :], [[4, 8], [0, 16]], 0, -1, **imp))
    c1 = one(g.iota(T.tI[:, :], [[1, 144]], -15, 0, **imp))
    c3 = one(g.iota(T.eE[0:96, :], [[4, 8], [0, 2], [32, 8]], 0, -1, **imp))

    def num(j):
        return T.tI[:, 15 + j:16 + j]

    v0 = event()
    add(v0, V.memset(T.L4[32:64, 0:8], 0))
    add(v0, V.memset(T.L4[64:128, 0:8], 0))
    wait(g, v0)
    g.wait_ge(T.sem.lL, 16)
    nH = send(T.LN[:, 0:8], T.L4[:, 0:8], T.sem.aH, T.sem.sH, [T.cores[(rank + n - 1) % n]])

    wait(V, c0)
    v1 = event()
    add(v1, V.tensor_scalar(T.cI[:, 4:5], T.cI[:, 0:1], 63, None, A.bitwise_and))
    add(v1, V.tensor_scalar(T.cI[:, 2:4], T.cI[:, 0:2], 15, None, A.bitwise_and))
    add(v1, V.tensor_scalar(T.cI[:, 5:6], T.cI[:, 0:1], 112, None, A.bitwise_and))
    wait(V, v1)
    cf = one(V.tensor_copy(T.cF[:, :], T.cI[:, :]))
    pcol, ccol, ycol, s16 = [T.cF[:, j:j + 1] for j in (0, 2, 4, 5)]
    cc = T.cF[:, 2:4]

    wait(S, c1, cf)
    q0 = event()
    add(q0, S.activation(T.cA[:, 0:1], ccol, ACT.Copy, scale=17.0))
    add(q0, S.activation(T.cA[:, 1:2], ccol, ACT.Copy, scale=-1.0))
    add(q0, S.activation(T.cA[:, 3:4], s16, ACT.Identity, scale=-17.0, bias=num(1)))
    add(q0, S.activation(T.cA[:, 2:3], ccol, ACT.Copy, scale=16.0))
    wait(S, q0)
    ql = one(S.activation(T.pL[:, :], T.tI[:, :], ACT.Abs, scale=17.0, bias=T.cA[:, 3:4]))
    wait(S, ql)
    bl = one(S.activation(T.BL[:, :], T.pL[:, :], ACT.Relu, scale=T.cA[:, 1:2], bias=T.cA[:, 0:1]))

    wait(V, c2)
    sr = event()
    for q in range(4):
        add(sr, V.tensor_scalar(T.RQ[0:32, 128 * q:128 * q + 128], T.eR[0:32, :], float(-q), None, A.is_equal))
    V.wait_ge(T.sem.lL, 16)
    lr = one(V.tensor_copy(T.L4h[0:32, :], T.L4[0:32, :]))
    wait(P, lr, sr)
    for q in range(4):
        ins = P.matmul(T.ps0[:, 128 * q:128 * q + 128], T.RQ[0:32, 128 * q:128 * q + 128], T.L4h[0:32, :], True, True)
    pl = one(ins)

    wait(V, cf, c1)
    i64 = one(V.tensor_scalar(T.I64[:, :], T.tI[:, 15:79], ycol, None, A.is_equal))
    cvs = []
    for j in range(4):
        V.wait_ge(T.sem["lK%d" % j], 16)
        cvs.append(one(V.tensor_scalar(T.KB[:, :, 16 * j:16 * j + 16], T.KR[:, j, :, :], -256.0, None, A.add)))
    wait(P, i64, *cvs)
    tr = {}
    tb = {0: T.ps5, 2: T.ps7, 1: T.ps6, 3: T.ps4}
    for h in (0, 2, 1, 3):
        for b in (h, h + 4):
            for a in (0, 64):
                ins = P.matmul(tb[h][a:a + 64, b // 4:128:2], T.KB[a:a + 64, b, :], T.I64[a:a + 64, :], True, True)
        tr[h] = one(ins)
    V.wait_ge(T.sem.lT, 48)
    tf = one(V.tensor_copy(T.ps3[0:96, 0:128], T.T4[0:96, :]))
    wait(V, pl)
    oa = one(V.tensor_scalar(T.OH[:, 0:272], T.ps0[:, 0:272], ccol, None, A.is_equal))
    bs = one(V.tensor_scalar(T.B[:, :], T.tI[:, :], s16, None, A.is_equal))
    se = []

    def selectors(h):
        wait(V, c3)
        e = event()
        for q in (2 * h, 2 * h + 1):
            add(e, V.tensor_scalar(T.EQ[0:96, 128 * q:128 * q + 128], T.eE[0:96, :], float(-q), None, A.is_equal))
        se.append(e)

    selectors(0)
    we = event()
    for h in (0, 2, 3):
        if h == 3:
            wait(S, tf)
            hp = one(S.activation(T.X4[0:96, :], T.ps3[0:96, 0:128], ACT.Copy))
        wait(S, tr[h])
        add(we, S.activation(T.W[:, w0 + h:w1:4], tb[h][:, 0:128], ACT.Copy))
    wait(S, hp)
    fp = one(S.activation(T.X4[64:96, :], T.X4[64:96, :], ACT.Sign))
    wait(S, bs, q0)
    bc = event()
    add(bc, S.activation(T.BC[:, :], T.B[:, :], ACT.Copy, scale=ccol))
    add(bc, S.activation(T.BD[:, :], T.B[:, :], ACT.Copy, scale=T.cA[:, 2:3]))
    wait(V, tr[1])
    r1 = one(V.tensor_scalar(T.R1[:, 0:1], tb[1][:, 0:1], 256.0, None, A.add))
    wc = one(V.tensor_copy(T.W[:, w0 + 1:w1:4], tb[1][:, 0:128]))
    wait(V, hp, tf)
    qp = one(V.tensor_tensor(T.X4[32:64, :], T.ps3[32:64, 0:128], T.X4[32:64, :], A.subtract))
    wait(V, r1, we, wc)
    d2 = one(V.tensor_scalar(T.D2[:, :], T.W[:, w0:w1].indirect(T.R1[:, 0:1]), 256.0, None, A.add))
    v2 = one(V.tensor_scalar(T.cA[:, 6:8], cc, 8.0, None, A.is_lt))
    wait(V, d2)
    t3 = one(V.tensor_copy(T.T3[:, t0:t1], T.W[:, w0:w1].indirect(T.D2[:, 4 * rank:4 * rank + 4])))
    wait(g, t3)
    nT = send(T.T3[:, t0:t1], T.T3[:, t0:t1], T.sem.aT, T.sem.sT, others)
    wait(g, we, wc)
    nW = send(T.W[:, w0:w1], T.W[:, w0:w1], T.sem.aW, T.sem.sW, others)

    selectors(1)
    ob = one(V.tensor_scalar(T.OH[:, 272:512], T.ps0[:, 272:512], ccol, None, A.is_equal))
    V.wait_ge(T.sem.aH, nH)
    ln = one(V.tensor_copy(T.Lnh[0:32, :], T.LN[0:32, :]))
    acc = [T.ps1, T.ps2]

    def pairs(s):
        a = 256 * s
        for x in range(1, 16):
            P.matmul(acc[s][:, 0:16], T.BL[:, 15 - x:143 - x], T.OH[:, a + x:a + 256:16], x == 1, False)
        wait(P, bc)
        P.matmul(acc[s][:, 0:16], T.BD[:, 15:143], T.OH[:, a:a + 256:16], False, False)
        return one(P.matmul(acc[s][:, 0:16], T.BC[:, 0:128], T.OH[:, a + 16:a + 257:16], False, True))

    wait(P, oa, bl)
    pairs0 = pairs(0)
    wait(P, hp, fp, qp, we)
    ti, pt = [T.ps5, T.ps3], []
    for h in range(2):
        wait(P, se[h])
        for q in range(2):
            c = 256 * h + 128 * q
            ins = P.matmul(ti[h][:, 128 * q:128 * q + 128], T.EQ[0:96, c:c + 128], T.X4[0:96, :], True, True)
        pt.append(one(ins))
    wait(P, ln)
    ph = one(P.matmul(T.ps4[:, 256:264], T.RQ[0:32, 0:128], T.Lnh[0:32, :], True, True))

    ls, bw = {}, {}

    def copylist(k, s):
        c = 32 * k - 64 + 16 * s
        if k == 2:
            ls[k, s] = one(V.tensor_copy(T.LS[:, c:c + 16], acc[s][:, 0:16]))
        else:
            ls[k, s] = one(V.tensor_scalar(T.LS[:, c:c + 16], acc[s][:, 0:16], 256.0 - 66048.0, None, A.add))

    def owners(s):
        wait(V, ls[2, s])
        bw[s] = one(V.tensor_scalar(T.bw[:, 16 * s:16 * s + 16], T.LS[:, 16 * s:16 * s + 16], 8224.5, None, A.add))

    wait(V, pairs0)
    copylist(2, 0)
    ident = one(V.tensor_scalar(T.ID[:, :], T.tI[:, 15:143], pcol, 8.0, A.is_equal, A.mult))
    owners(0)
    wait(V, ph)
    ohn = one(V.tensor_scalar(T.OH[:, 512:520], T.ps4[:, 256:264], ccol, None, A.is_equal))
    wait(P, ob, ohn)
    pairs1 = pairs(1)
    v3 = event()
    add(v3, V.tensor_scalar(T.cA[:, 8:10], cc, 2.0, None, A.is_equal))
    add(v3, V.tensor_scalar(T.cA[:, 10:12], cc, 2.0, None, A.is_lt))

    iw = event()
    for h in range(2):
        wait(S, pt[h])
        add(iw, S.activation(T.IDW[:, w0 + 256 * h:w0 + 256 * h + 256], ti[h][:, 0:256], ACT.Copy))
    wait(S, iw, r1, d2, v2)
    ii = event()
    add(ii, S.activation(T.I1[:, :], T.IDW[:, w0:w1].indirect(T.R1[:, 0:1]), ACT.Copy, scale=T.cA[:, 7:8]))
    add(ii, S.activation(T.I2[:, :], T.IDW[:, w0:w1].indirect(T.D2[:, 4 * rank:4 * rank + 4]), ACT.Copy, scale=T.cA[:, 6:7]))
    wait(S, ii)
    kt = event()
    for j in range(4):
        add(kt, S.activation(T.KT[:, t0 + 16 * j:t0 + 16 * j + 16], T.I2[:, 16 * j:16 * j + 16], ACT.Identity,
                             bias=T.I1[:, 4 * rank + j:4 * rank + j + 1]))
    wait(g, kt)
    nK = send(T.KT[:, t0:t1], T.KT[:, t0:t1], T.sem.aK, T.sem.sK, others)
    wait(g, iw)
    nI = send(T.IDW[:, w0:w1], T.IDW[:, w0:w1], T.sem.aI, T.sem.sI, others)
    q1 = one(S.activation(T.cA[:, 4:5], s16, ACT.Identity, scale=-0.5, bias=num(8)))
    wait(S, q1, v3)
    pa = event()
    add(pa, S.activation(T.pA[:, 0:64], T.tI[:, 0:64], ACT.Abs, bias=T.cA[:, 4:5]))
    add(pa, S.activation(T.pA[:, 64:136], T.tI[:, 0:72], ACT.Abs, bias=T.cA[:, 4:5]))
    q4 = event()
    add(q4, S.activation(T.cA[:, 12:13], T.cA[:, 8:9], ACT.Identity, scale=65536.0, bias=T.cA[:, 10:11]))
    add(q4, S.activation(T.cA[:, 13:14], T.cA[:, 9:10], ACT.Identity, scale=65536.0, bias=T.cA[:, 11:12]))
    add(q4, S.activation(T.cA[:, 15:16], T.cA[:, 8:9], ACT.Copy, scale=393216.0))
    add(q4, S.activation(T.cA[:, 16:17], T.cA[:, 8:9], ACT.Copy, scale=6.0))
    sc = one(S.activation(T.cA[:, 18:24], T.tI[:, 15:21], ACT.Identity, scale=T.cA[:, 8:9], bias=num(1)))
    wait(S, pa)
    pp = one(S.activation(T.pP[:, :], T.pA[:, :], ACT.Relu, scale=-1.0, bias=num(1)))
    wait(S, pp, q4)
    sel = event()
    add(sel, S.activation(T.D[:, :], T.pP[:, :], ACT.Copy, scale=T.cA[:, 12:13]))
    add(sel, S.activation(T.D1[:, :], T.pP[:, :], ACT.Copy, scale=T.cA[:, 13:14]))
    add(sel, S.activation(T.D6[:, 0:64], T.pP[:, 0:64], ACT.Copy, scale=T.cA[:, 15:16]))
    add(sel, S.activation(T.D6[:, 64:136], T.pP[:, 64:136], ACT.Copy, scale=T.cA[:, 16:17]))
    add(sel, S.activation(T.DI[:, :], T.pP[:, 64:136], ACT.Copy, scale=T.cA[:, 10:11]))

    bank = {1: T.ps4, 2: T.ps5, 3: T.ps6, 4: T.ps7, 5: T.ps3}
    gat, gid, idp, ky = {}, {}, {}, {}

    def idsum(out, m, D, G, bs):
        for b in bs:
            ins = P.matmul(out[0:m, 0:64], D[:, 7 - b:7 - b + m], G[:, 64 * b:64 * b + 64], b == 0, b == 7)
        return ins

    def idstep(m):
        k = max(m, 2)
        wait(P, gid[k], sel)
        if m == 1:
            wait(P, ohn, r1, we, wc, iw)
        idp[m] = one(idsum(bank[m], 128, T.D1 if m == 1 else T.D, T["G%d" % k], range(8)))

    def keystep(k):
        wait(V, idp[k])
        o = T.keyI if k == 5 else T.key
        if k == 1:
            ky[k] = one(V.tensor_copy(o[:, :], bank[k][:, 0:64]))
        else:
            wait(V, ky[k - 1])
            ky[k] = one(V.tensor_tensor(o[:, :], T.key[:, :], bank[k][:, 0:64], A.max))

    def gather(k, s):
        c = 32 * k - 96 + 16 * s
        wait(V, ls[k - 1, s])
        gat[k, s] = one(V.tensor_tensor(T["RM%d" % s][:, :], (T.T3 if k == 3 else T.W)[:, :].indirect(T.LS[:, c:c + 16]),
                                        T.OH[:, 256 * s + k - 1:256 * s + k + 255], A.mult))

    def idgather(k):
        wait(S, ls[k, 0], ls[k, 1])
        gid[k] = one(S.activation(T["G%d" % k][:, :], (T.KT if k == 2 else T.IDW)[:, :].indirect(T.LS[:, 32 * k - 64:32 * k - 32]),
                                  ACT.Copy, scale=T.cA[:, 17 + k:18 + k]))

    def addowners(s, start, stop):
        if start is not stop and stop:
            wait(P, bw[s], ident)
        return P.matmul(acc[s][:, 0:16], T.ID[:, :], T.bw[:, 16 * s:16 * s + 16], start, stop)

    V.wait_ge(T.sem.aT, nT * len(others))
    wait(V, t3, oa)
    gather(3, 0)
    wait(V, pairs1)
    copylist(2, 1)
    wait(V, ob, ohn)
    gather(3, 1)
    owners(1)
    S.wait_ge(T.sem.aK, nK * len(others))
    wait(S, sc, kt)
    idgather(2)
    S.wait_ge(T.sem.aI, nI * len(others))
    wait(P, bs)
    begin = {(5, 0): 1, (5, 1): 2, (6, 1): 3}
    keys = {(5, 1): 1, (6, 0): 2, (6, 1): 3}
    for k in range(3, 7):
        pm = []
        for s in range(2):
            if (k, s) in begin:
                idstep(begin[k, s])
            wait(P, ls[k - 1, s])
            if k > 3:
                addowners(s, True, False)
            wait(P, gat[k, s])
            for x in range(16):
                ins = P.matmul(acc[s][:, 0:16], T.B[:, 15 - x:143 - x], T["RM%d" % s][:, x:256:16],
                               k == 3 and x == 0, k > 3 and x == 15)
            if k == 3:
                ins = addowners(s, False, True)
            pm.append(one(ins))
        if k == 6:
            idstep(4)
            idstep(5)
        for s in range(2):
            c = 32 * k - 64 + 16 * s
            wait(V, pm[s])
            copylist(k, s)
            if (k, s) in keys:
                keystep(keys[k, s])
            if k < 6:
                if k == 3 and s == 0:
                    V.wait_ge(T.sem.aW, nW * len(others))
                gather(k + 1, s)
            elif s == 0:
                V.wait_ge(T.sem.aI, nI * len(others))
                wait(V, iw, ls[6, 0])
                i0 = one(V.tensor_copy(T.G6[:, 0:256], T.IDW[:, :].indirect(T.LS[:, c:c + 16])))
            else:
                wait(S, ls[6, 1])
                wait(V, ls[6, 1])
                i1 = one(V.tensor_copy(T.G6[:, 256:352], T.IDW[:, :].indirect(T.LS[:, c:c + 6])))
                i2 = one(S.activation(T.G6[:, 352:512], T.IDW[:, :].indirect(T.LS[:, c + 6:c + 16]), ACT.Copy))
        if k < 6:
            idgather(k)
    zb, ib = T.ps0, T.ps1
    wait(P, i0)
    idsum(zb, 128, T.D6, T.G6, range(4))
    idsum(ib, 64, T.DI, T.G6, range(4))
    wait(P, i1, i2)
    pz = one(idsum(zb, 128, T.D6, T.G6, range(4, 8)))
    pi = one(idsum(ib, 64, T.DI, T.G6, range(4, 8)))
    keystep(4)
    keystep(5)
    wait(V, ky[5])
    k5 = event()
    add(k5, V.tensor_scalar(T.idI[0:64, :], T.keyI[0:64, :], 65535, None, A.bitwise_and))
    add(k5, V.tensor_scalar(T.kI[64:128, :], T.keyI[64:128, :], 16, None, A.arith_shift_right))
    wait(V, pz, k5)
    ue = one(V.tensor_tensor(T.u[0:64, :], T.idI[0:64, :], zb[0:64, 0:64], A.subtract))
    ol = one(V.tensor_tensor(T.OL[64:128, :], T.kI[64:128, :], zb[64:128, 0:64], A.max))
    wait(V, pi, ue)
    od = one(V.tensor_tensor(T.OD[0:64, :], T.u[0:64, :], ib[0:64, 0:64], A.max))
    wait(S, ol)
    S.dma_start(T.ylen[:, :], T.OL[64:128, :]).then_inc(T.sem.oY, 16)
    wait(Y, od)
    Y.dma_start(T.yid[:, :], T.OD[0:64, :]).then_inc(T.sem.oY, 16)
    g.wait_ge(T.sem.sH, nH)
    g.wait_ge(T.sem.sT, nT)
    g.wait_ge(T.sem.sW, nW)
    g.wait_ge(T.sem.sI, nI)
    g.wait_ge(T.sem.sK, nK)
    for e in evs:
        if not e[2]:
            wait(g, e)
    g.wait_ge(T.sem.oY, 32)
